import numpy as np
import ml_dtypes


def mxq(x, axis, fmt="e4m3"):
    dtype, down = {"e4m3": (ml_dtypes.float8_e4m3fn, 7), "e5m2": (ml_dtypes.float8_e5m2, 14)}[fmt]
    v = np.moveaxis(np.asarray(x, np.float32).astype(ml_dtypes.bfloat16).astype(np.float64), axis, -1)
    blocks = v.reshape(v.shape[:-1] + (-1, 32))
    amax = np.abs(blocks).max(-1, keepdims=True)
    byte = np.maximum(np.where(amax > 0, np.frexp(amax)[1] - 1 + 127, 0) - down, 1)
    scale = np.exp2(byte - 127.0)
    codes = (blocks / scale).astype(np.float32).astype(dtype).astype(np.float64)
    return np.moveaxis((codes * scale).reshape(v.shape), -1, axis)


WIDE = False


def mx_kscale(k):
    if not WIDE:
        return np.ones(k)
    levels = np.array([10, -10, 5, -5, 0])
    if k % 512:
        return np.exp2(np.random.permutation(np.resize(levels, k // 32))).repeat(32)
    a = np.empty((k // 512, 16))
    for p in range(k // 512):
        a[p, :8] = np.random.permutation(np.resize(levels, 8))
        for g in range(8):
            far = levels[np.abs(levels - a[p, g]) >= 10]
            a[p, g + 8] = far[np.random.randint(len(far))]
    return np.exp2(a.ravel()).repeat(32)


BF16 = ml_dtypes.bfloat16


def bf(x):
    return np.asarray(x, np.float32).astype(BF16)


def f64(x):
    return np.asarray(x).astype(np.float64)


E2M1 = np.array([0.0, 0.5, 1.0, 1.5, 2.0, 3.0, 4.0, 6.0, -0.0, -0.5, -1.0, -1.5, -2.0, -3.0, -4.0, -6.0])


def pack_weight(w, fmt):
    k, n = w.shape
    w = f64(bf(w)).reshape(k // 32, 32, n)
    amax = np.abs(w).max(1)
    if fmt == "e4m3":
        byte = np.frexp(amax)[1] - 1 + 127 - 7
    else:
        mant, ex = np.frexp(amax / 6.0)
        byte = np.where(mant > 0.5, ex, ex - 1) + 127
    byte = np.clip(np.where(amax > 0, byte, 1), 1, 254)
    scaled = (w * np.exp2(127.0 - byte)[:, None, :]).reshape(k, n).astype(np.float32)
    by_word = np.ascontiguousarray(scaled.reshape(k // 512, 128, 4, n).transpose(0, 1, 3, 2))
    if fmt == "e4m3":
        words = by_word.astype(ml_dtypes.float8_e4m3fn).view(np.uint8)
    else:
        c = by_word.astype(ml_dtypes.float4_e2m1fn).view(np.uint8) & 0xF
        words = c[..., 0::2] | (c[..., 1::2] << 4)
    return np.ascontiguousarray(words), np.ascontiguousarray(byte.astype(np.uint8).reshape(k // 512, 16, n))


def unpack_weight(words, scales, fmt):
    g, p, n, _ = words.shape
    if fmt == "e4m3":
        vals = np.ascontiguousarray(words).view(ml_dtypes.float8_e4m3fn).astype(np.float64)
    else:
        nib = np.empty((g, p, n, 4), np.uint8)
        nib[..., 0::2] = words & 0xF
        nib[..., 1::2] = words >> 4
        vals = E2M1[nib]
    vals = vals * np.repeat(np.exp2(scales.astype(np.float64) - 127.0), 8, axis=1)[..., None]
    return vals.transpose(0, 1, 3, 2).reshape(g * 512, n)
def pack4(w):
    words, scales = pack_weight(w, "e2m1")
    return words.reshape(words.shape[0], 128, -1), scales


def unpack4(words, scales):
    return unpack_weight(words.reshape(words.shape[0], 128, -1, 2), scales, "e2m1")


def planes(Y):
    n, m = Y.shape
    b = f64(bf(Y)).reshape(n // 32, 32, m)
    amax = np.abs(b).max(1)
    byte = np.clip(np.where(amax > 0, np.frexp(amax)[1] - 1 + 127 - 7, 1), 1, 254)
    codes = (b * np.exp2(127.0 - byte)[:, None, :]).reshape(n, m).astype(np.float32).astype(ml_dtypes.float8_e4m3fn).view(np.uint8)
    words = codes.reshape(n // 512, 128, 4, m).transpose(0, 1, 3, 2)
    return np.ascontiguousarray(words), np.ascontiguousarray(byte.astype(np.uint8).reshape(n // 512, 16, m))


S, D, R = 768, 1024, 1536

def setup_inputs():
    rn = np.random.randn
    s, t = mx_kscale(D), mx_kscale(R)
    spread = np.exp(0.8 * rn(D))
    z_words, z_scales = pack_weight(rn(D, S) / s[:, None], "e4m3")
    b_words, b_scales = pack4(rn(D, R) / np.sqrt(D) * s[:, None] * t[None, :])
    return {
        "z_words": z_words, "z_scales": z_scales,
        "b_words": b_words, "b_scales": b_scales,
        "mix": bf(4.0 * rn(D, D) / np.sqrt(D) / s[None, :]),
        "lower": bf(-(0.3 + 0.6 * np.abs(rn(R))) * t),
        "upper": bf((0.3 + 0.6 * np.abs(rn(R))) * t),
        "react_weight": bf(np.exp(0.3 * rn(R)) / t**2),
        "gain": bf(0.2 * spread),
        "step": bf(0.5 * spread * np.exp(0.2 * rn(D))),
        "moves": bf(rn(S, D)),
    }

def reference(z_words, z_scales, b_words, b_scales, mix, lower, upper, react_weight, gain, step, moves):
    Z = unpack_weight(z_words, z_scales, "e4m3")
    B = unpack4(b_words, b_scales)
    V = np.minimum(np.maximum(Z.T @ B, f64(lower)), f64(upper))
    Q = (mxq(f64(mix), 1, "e4m3") @ B) * f64(react_weight)
    P = mxq(V, 1, "e4m3") @ mxq(Q, 1, "e4m3").T
    y = P * f64(gain) + f64(step) * f64(moves)
    Y = y.T
    words, scales = planes(Y)
    return y, words, scales

@@ -1,0 +1,433 @@
+from contextlib import ExitStack
+
+import concourse.mybir as mybir
+from concourse.masks import make_identity
+
+S, D, R = 768, 1024, 1536
+FLOPS = 2 * S * D * R + 2 * D * D * R + 2 * S * R * D
+
+F32 = mybir.dt.float32
+BF16 = mybir.dt.bfloat16
+I32 = mybir.dt.int32
+U32 = mybir.dt.uint32
+U8 = mybir.dt.uint8
+FP8X4 = mybir.dt.float8_e4m3fn_x4
+FP4X4 = mybir.dt.float4_e2m1fn_x4
+ALU = mybir.AluOpType
+COPY = mybir.ActivationFunctionType.Copy
+
+P = 128
+SLOTS = 4
+PASS = 512
+DG = D // PASS
+RG = R // PASS
+BANK = 512
+S_MAIN = 512
+S_TAIL = S - S_MAIN
+B_SCALE_PARTS = ((0, 1), (1, 2))
+
+
+def tile_clipped_flux_reprojection_k4_kernel(
+    tc, z_words, z_scales, b_words, b_scales, mix, lower, upper, react_weight, gain, step, moves,
+    out_0, out_1, out_2,
+):
+    nc = tc.nc
+    with ExitStack() as ctx:
+        keep = ctx.enter_context(tc.tile_pool(name="keep", bufs=1))
+        work = ctx.enter_context(tc.tile_pool(name="work", bufs=2))
+        psum = ctx.enter_context(tc.psum_pool(name="psum", bufs=8))
+        ctx.enter_context(tc.manual_schedule())
+
+        def kept(name, shape, dtype):
+            return keep.tile(shape, dtype, name=name, align_bytes=64)
+
+        def bank(shape):
+            return psum.tile(shape, F32, name="bank")
+
+        ident = kept("ident", [P, P], F32)
+        warm = kept("warm", [P, 8], F32)
+        vec_rows = kept("vec_rows", [P, PASS], BF16)
+        vec_sorted = kept("vec_sorted", [P, SLOTS, P], F32)
+        react = kept("react", [P, SLOTS, 16], F32)
+        gain_sb = kept("gain_sb", [P, DG, SLOTS], BF16)
+        step_bf = kept("step_bf", [P, DG, SLOTS], BF16)
+        step_sb = kept("step_sb", [P, DG, SLOTS], F32)
+        mix_raw = [kept("mix_raw%d" % h, [P, SLOTS, D], BF16) for h in range(DG)]
+        moves_raw = kept("moves_raw", [P, S // P, D], BF16)
+        b_raw = [kept("b_raw%d" % g, [P, DG * 2 * PASS], U8) for g in range(RG)]
+        b_codes = [kept("b_codes%d" % g, [P, SLOTS, DG * 2 * P], U8) for g in range(RG)]
+        bs_raw = [kept("bs_raw%d" % i, [P, DG * PASS * n], U8) for i, (g0, n) in enumerate(B_SCALE_PARTS)]
+        b_sc = [kept("b_sc%d" % i, [P, SLOTS, DG * P * n], U8) for i, (g0, n) in enumerate(B_SCALE_PARTS)]
+        z_codes = kept("z_codes", [P, DG, S], U32)
+        z_sc = kept("z_sc", [P, DG, S], U8)
+        mix_codes = kept("mix_codes", [P, DG, D], U32)
+        mix_sc = kept("mix_sc", [P, DG, D], U8)
+        q_codes = kept("q_codes", [P, RG, D], U32)
+        q_sc = kept("q_sc", [P, RG, D], U8)
+        v_codes = kept("v_codes", [P, RG, S], U32)
+        v_sc = kept("v_sc", [P, RG, S], U8)
+        y_codes = kept("y_codes", [P, DG, S], U32)
+        y_sc = kept("y_sc", [P, DG, S], U8)
+        shift = kept("shift", [P, DG, SLOTS, S], F32)
+        mix_grouped = {}
+        live = {}
+
+        def interleave(dst, src, copy=nc.vector.tensor_copy):
+            copy(
+                out=dst.rearrange("p (c i t) -> p c t i", i=4, t=SLOTS),
+                in_=src.rearrange("p t (c i) -> p c t i", i=4),
+            )
+
+        def load_scales(dst, src):
+            for q in range(4):
+                nc.sync.dma_start(
+                    out=dst[32 * q : 32 * q + 4].bitcast(I32),
+                    in_=src[:, 4 * q : 4 * q + 4, :].bitcast(I32).rearrange("k q n -> q k n"),
+                )
+
+        def load_b(g):
+            nc.sync.dma_start(
+                out=b_raw[g][:].bitcast(I32).rearrange("p (k n) -> p k n", k=DG),
+                in_=b_words[:, :, 2 * PASS * g : 2 * PASS * (g + 1)].bitcast(I32).rearrange("k p n -> p k n"),
+            )
+
+        def mix_rows(h):
+            return mix[PASS * h : PASS * (h + 1), :].rearrange("(p t) k -> p t k", t=SLOTS)
+
+        def sort_b(g):
+            nc.vector.tensor_copy(
+                out=b_codes[g][:].bitcast(I32).rearrange("p t (m j) -> p t m j", j=4),
+                in_=b_raw[g][:].bitcast(I32).rearrange("p (m t j) -> p t m j", t=SLOTS, j=4),
+            )
+
+        def load_b_scales(i):
+            g0, n = B_SCALE_PARTS[i]
+            load_scales(bs_raw[i][:].rearrange("p (k n) -> p k n", k=DG), b_scales[:, :, PASS * g0 : PASS * (g0 + n)])
+
+        def sort_b_scales(i):
+            nc.vector.tensor_copy(
+                out=b_sc[i][:].bitcast(I32).rearrange("p t (m j) -> p t m j", j=2),
+                in_=bs_raw[i][:].bitcast(I32).rearrange("p (m t j) -> p t m j", t=SLOTS, j=2),
+            )
+
+        def sort_vectors():
+            nc.vector.tensor_copy(
+                out=vec_sorted[:].rearrange("p t (b i) -> p t b i", i=8),
+                in_=vec_rows[:].rearrange("p (b t i) -> p t b i", t=SLOTS, i=8),
+            )
+
+        def turn_vectors():
+            acc = bank([P, SLOTS, P])
+            for t in range(SLOTS):
+                nc.tensor.transpose(acc[:, t, :], vec_sorted[:, t, :], ident[:])
+            nc.vector.tensor_copy(out=react[:], in_=acc[:, :, 0:16])
+
+        def turn_mix(h, t):
+            if t == 0:
+                mix_grouped[h] = keep.tile([P, DG, SLOTS * PASS], BF16, name="mix_grouped", align_bytes=64)
+            acc = bank([P, DG, 2, P])
+            words = mix_raw[h][:, t, :].bitcast(F32)
+            for k in range(DG):
+                for u in range(2):
+                    nc.tensor.transpose(acc[:, k, u, :], words[:, 256 * k + u : 256 * (k + 1) : 2], ident[:])
+            dst = mix_grouped[h][:].bitcast(F32).rearrange("p k (c u) -> p k c u", u=2)
+            nc.scalar.copy(out=dst[:, :, P * t : P * (t + 1), :], in_=acc[:].rearrange("p k u c -> p k c u"))
+
+        def quant_mix(h, k, c0, n):
+            cols = slice(PASS * h + c0, PASS * h + c0 + n)
+            nc.vector.quantize_mx(
+                out=mix_codes[:, k, cols].bitcast(FP8X4),
+                scales=mix_sc[:, k, cols],
+                in_=mix_grouped[h][:, k, SLOTS * c0 : SLOTS * (c0 + n)],
+            )
+
+        def times_b(dst, g, t, codes, scales, cols):
+            part = min(g, 1)
+            g0, n = B_SCALE_PARTS[part]
+            for k in range(DG):
+                m = k * n + g - g0
+                nc.tensor.matmul_mx(
+                    out=dst,
+                    lhsT=b_codes[g][:, t, 2 * P * k : 2 * P * (k + 1)].bitcast(FP4X4),
+                    lhsT_scale=b_sc[part][:, t, P * m : P * (m + 1)],
+                    rhs=codes[:, k, cols].bitcast(FP8X4),
+                    rhs_scale=scales[:, k, cols],
+                    start=(k == 0),
+                    stop=(k == DG - 1),
+                )
+
+        def q_product(h, g):
+            rows = work.tile([P, SLOTS, PASS], BF16, name="q_rows", align_bytes=64)
+            live["q_rows", h, g] = rows
+            for t in range(SLOTS):
+                acc = bank([P, BANK])
+                times_b(acc[:], g, t, mix_codes, mix_sc, slice(PASS * h, PASS * (h + 1)))
+                nc.scalar.activation(out=rows[:, t, :], in_=acc[:], func=COPY, scale=react[:, t, g : g + 1])
+
+        def q_group(h, g):
+            grouped = work.tile([P, SLOTS * PASS], BF16, name="q_grouped", align_bytes=64)
+            live["q_grouped", h, g] = grouped
+            interleave(grouped[:], live["q_rows", h, g][:])
+
+        def q_quant(h, g):
+            cols = slice(PASS * h, PASS * (h + 1))
+            nc.vector.quantize_mx(
+                out=q_codes[:, g, cols].bitcast(FP8X4), scales=q_sc[:, g, cols], in_=live["q_grouped", h, g][:]
+            )
+
+        def clip(dst, src, g, t):
+            nc.vector.tensor_scalar(
+                out=dst, in0=src,
+                scalar1=react[:, t, RG + g : RG + g + 1], scalar2=react[:, t, 2 * RG + g : 2 * RG + g + 1],
+                op0=ALU.max, op1=ALU.min,
+            )
+
+        def v_main(g):
+            rows = work.tile([P, SLOTS, S_MAIN], BF16, name="v_rows", align_bytes=64)
+            live["v_rows", g] = rows
+            for t in range(SLOTS):
+                acc = bank([P, BANK])
+                times_b(acc[:], g, t, z_codes, z_sc, slice(0, S_MAIN))
+                nc.scalar.copy(out=rows[:, t, :], in_=acc[:])
+
+        def v_tail(g):
+            for pair in range(2):
+                acc = bank([P, 2, S_TAIL])
+                live["v_tail_acc", g, pair] = acc
+                for e in range(2):
+                    for c0 in range(0, S_TAIL, P):
+                        times_b(acc[:, e, c0 : c0 + P], g, 2 * pair + e, z_codes, z_sc,
+                                slice(S_MAIN + c0, S_MAIN + c0 + P))
+
+        def v_tail_clip(g):
+            rows = work.tile([P, SLOTS, S_TAIL], BF16, name="v_tail_rows", align_bytes=64)
+            live["v_clipped", g, 1] = rows
+            for t in range(SLOTS):
+                clip(rows[:, t, :], live["v_tail_acc", g, t // 2][:, t % 2, :], g, t)
+
+        def v_main_clip(g):
+            rows = work.tile([P, SLOTS, S_MAIN], BF16, name="v_main_rows", align_bytes=64)
+            live["v_clipped", g, 0] = rows
+            for t in range(SLOTS):
+                clip(rows[:, t, :], live["v_rows", g][:, t, :], g, t)
+
+        def v_group(g, part):
+            n = (S_MAIN, S_TAIL)[part]
+            grouped = work.tile([P, SLOTS * n], BF16, name="v_grouped%d" % part, align_bytes=64)
+            live["v_grouped", g, part] = grouped
+            interleave(grouped[:], live["v_clipped", g, part][:])
+
+        def v_quant(g, part):
+            cols = (slice(0, S_MAIN), slice(S_MAIN, S))[part]
+            nc.vector.quantize_mx(
+                out=v_codes[:, g, cols].bitcast(FP8X4), scales=v_sc[:, g, cols], in_=live["v_grouped", g, part][:]
+            )
+
+        def scale_moves(h, u, s0, n, acc):
+            pairs = acc.bitcast(BF16).rearrange("p (s e) -> p e s", e=2)
+            for e in range(2):
+                t = 2 * u + e
+                nc.scalar.activation(
+                    out=shift[:, h, t, s0 : s0 + n], in_=pairs[:, e, :], func=COPY, scale=step_sb[:, h, t : t + 1]
+                )
+
+        def turn_moves_into(dst, h, u, j):
+            words = moves_raw[:, j, :].bitcast(F32)
+            nc.tensor.transpose(dst, words[:, 256 * h + u : 256 * (h + 1) : 2], ident[:])
+
+        def turn_moves_main(h, u):
+            acc = bank([P, BANK])
+            for j in range(S_MAIN // P):
+                turn_moves_into(acc[:, P * j : P * (j + 1)], h, u, j)
+            scale_moves(h, u, 0, S_MAIN, acc[:])
+
+        def turn_moves_tail(h):
+            acc = bank([P, 2, S_TAIL])
+            for u in range(2):
+                for j in range(S_TAIL // P):
+                    turn_moves_into(acc[:, u, P * j : P * (j + 1)], h, u, S_MAIN // P + j)
+            for u in range(2):
+                scale_moves(h, u, S_MAIN, S_TAIL, acc[:, u, :])
+
+        def p_product(h, s0, n, per_bank):
+            y_t = work.tile([P, SLOTS, n], F32, name="y_t", align_bytes=64, bufs=3)
+            live["y_t", h, s0] = y_t
+            cols = slice(s0, s0 + n)
+            for t0 in range(0, SLOTS, per_bank):
+                acc = bank([P, per_bank, n])
+                for e in range(per_bank):
+                    d = slice(PASS * h + P * (t0 + e), PASS * h + P * (t0 + e + 1))
+                    for g in range(RG):
+                        nc.tensor.matmul_mx(
+                            out=acc[:, e, :],
+                            lhsT=q_codes[:, g, d].bitcast(FP8X4), lhsT_scale=q_sc[:, g, d],
+                            rhs=v_codes[:, g, cols].bitcast(FP8X4), rhs_scale=v_sc[:, g, cols],
+                            start=(g == 0), stop=(g == RG - 1),
+                        )
+                for e in range(per_bank):
+                    t = t0 + e
+                    nc.vector.scalar_tensor_tensor(
+                        out=y_t[:, t, :], in0=acc[:, e, :], scalar=gain_sb[:, h, t : t + 1],
+                        in1=shift[:, h, t, cols], op0=ALU.mult, op1=ALU.add,
+                    )
+
+        def y_group(h, s0, n, copy):
+            grouped = work.tile([P, SLOTS * n], BF16, name="y_grouped", align_bytes=64)
+            live["y_grouped", h, s0] = grouped
+            interleave(grouped[:], live["y_t", h, s0][:], copy)
+
+        def y_quant(h, s0, n):
+            cols = slice(s0, s0 + n)
+            nc.vector.quantize_mx(
+                out=y_codes[:, h, cols].bitcast(FP8X4), scales=y_sc[:, h, cols], in_=live["y_grouped", h, s0][:]
+            )
+
+        def store_words(h, s0, n):
+            nc.sync.dma_start(
+                out=out_1[h].rearrange("p s t -> p (s t)").bitcast(I32)[:, s0 : s0 + n],
+                in_=y_codes[:, h, s0 : s0 + n].bitcast(I32),
+            )
+
+        def store_scales(h, queues):
+            for q in range(4):
+                queues[q].dma_start(
+                    out=out_2[h, 4 * q : 4 * q + 4, :].bitcast(I32),
+                    in_=y_sc[32 * q : 32 * q + 4, h, :].bitcast(I32),
+                )
+
+        def turn_y(h, s0, j0, count):
+            rows = work.tile([P, count, PASS], F32, name="y_rows", align_bytes=64, bufs=3)
+            for j in range(count):
+                acc = bank([P, SLOTS, P])
+                for t in range(SLOTS):
+                    c0 = P * (j0 + j)
+                    nc.tensor.transpose(acc[:, t, :], live["y_t", h, s0][:, t, c0 : c0 + P], ident[:])
+                nc.scalar.copy(
+                    out=rows[:, j, :].rearrange("s (p t) -> s p t", t=SLOTS), in_=acc[:].rearrange("s t p -> s p t")
+                )
+            r0 = s0 + P * j0
+            nc.sync.dma_start(
+                out=out_0[r0 : r0 + P * count, PASS * h : PASS * (h + 1)].rearrange("(j s) d -> s j d", s=P),
+                in_=rows[:],
+            )
+
+        make_identity(nc, ident[:])
+        nc.vector.memset(vec_rows[:], 0.0)
+        nc.vector.memset(warm[:], 0.0)
+        nc.vector.memset(bs_raw[0][:].bitcast(I32), 0)
+        nc.vector.memset(bs_raw[1][:].bitcast(I32), 0)
+        nc.vector.memset(z_sc[:].rearrange("p k n -> p (k n)").bitcast(I32), 0)
+        nc.scalar.activation(out=warm[:, 0:1], in_=warm[:, 1:2], func=COPY, scale=warm[:, 2:3])
+        for t in range(SLOTS):
+            nc.sync.dma_start(out=mix_raw[0][:, t, :], in_=mix_rows(0)[:, t, :])
+        for i, vec in enumerate((react_weight, lower, upper)):
+            nc.sync.dma_start(out=vec_rows[RG * i : RG * (i + 1), :], in_=vec.rearrange("(g r) -> g r", g=RG))
+        load_b(0)
+        load_b_scales(0)
+        load_b(1)
+        load_b_scales(1)
+        nc.sync.dma_start(out=z_codes[:].bitcast(I32), in_=z_words.rearrange("k p n t -> p k (n t)").bitcast(I32))
+        load_scales(z_sc[:], z_scales)
+        load_b(2)
+        nc.sync.dma_start(out=mix_raw[1][:], in_=mix_rows(1))
+        nc.sync.dma_start(out=gain_sb[:], in_=gain.rearrange("(h p t) -> p h t", h=DG, t=SLOTS))
+        nc.sync.dma_start(out=step_bf[:], in_=step.rearrange("(h p t) -> p h t", h=DG, t=SLOTS))
+        nc.sync.dma_start(out=moves_raw[:], in_=moves.rearrange("(j s) d -> s j d", s=P))
+
+        for t in range(SLOTS):
+            turn_mix(0, t)
+            if t == 2:
+                sort_vectors()
+            if t == 3:
+                sort_b(0)
+                sort_b_scales(0)
+            for k in range(DG):
+                quant_mix(0, k, P * t, P)
+        turn_vectors()
+        q_product(0, 0)
+        sort_b(1)
+        sort_b_scales(1)
+        q_product(0, 1)
+        q_group(0, 0)
+        sort_b(2)
+        q_quant(0, 0)
+        v_main(0)
+        q_group(0, 1)
+        v_tail(0)
+        nc.vector.tensor_copy(out=step_sb[:], in_=step_bf[:])
+        q_quant(0, 1)
+        v_main_clip(0)
+        v_tail_clip(0)
+        for t in range(SLOTS):
+            turn_mix(1, t)
+        v_group(0, 0)
+        v_group(0, 1)
+        v_quant(0, 0)
+        v_quant(0, 1)
+        q_product(0, 2)
+        for k in range(DG):
+            quant_mix(1, k, 0, PASS)
+        v_main(1)
+        q_group(0, 2)
+        v_tail(1)
+        v_main_clip(1)
+        q_quant(0, 2)
+        v_tail_clip(1)
+        q_product(1, 0)
+        v_group(1, 0)
+        v_group(1, 1)
+        v_quant(1, 0)
+        v_quant(1, 1)
+        v_main(2)
+        q_group(1, 0)
+        v_tail(2)
+        v_main_clip(2)
+        q_quant(1, 0)
+        v_tail_clip(2)
+        turn_moves_main(0, 0)
+        turn_moves_main(0, 1)
+        turn_moves_tail(0)
+        v_group(2, 0)
+        v_group(2, 1)
+        v_quant(2, 0)
+        v_quant(2, 1)
+        on_vector, on_scalar = nc.vector.tensor_copy, nc.scalar.copy
+        q_product(1, 1)
+        p_product(0, 0, 512, 1)
+        q_product(1, 2)
+        q_group(1, 1)
+        turn_moves_main(1, 0)
+        turn_moves_main(1, 1)
+        q_quant(1, 1)
+        q_group(1, 2)
+        p_product(0, 512, 256, 2)
+        q_quant(1, 2)
+        turn_y(0, 0, 0, 2)
+        turn_moves_tail(1)
+        y_group(0, 0, 512, on_vector)
+        turn_y(0, 0, 2, 2)
+        p_product(1, 0, 256, 2)
+        y_quant(0, 0, 512)
+        y_group(0, 512, 256, on_vector)
+        turn_y(0, 512, 0, 2)
+        p_product(1, 256, 256, 2)
+        y_quant(0, 512, 256)
+        store_words(0, 0, 768)
+        store_scales(0, [nc.sync] * 4)
+        y_group(1, 0, 256, on_scalar)
+        turn_y(1, 0, 0, 2)
+        p_product(1, 512, 128, 4)
+        y_quant(1, 0, 256)
+        y_group(1, 256, 256, on_vector)
+        turn_y(1, 256, 0, 2)
+        p_product(1, 640, 128, 1)
+        y_quant(1, 256, 256)
+        store_words(1, 0, 512)
+        y_group(1, 512, 128, on_vector)
+        y_group(1, 640, 128, on_vector)
+        y_quant(1, 512, 128)
+        y_quant(1, 640, 128)
+        turn_y(1, 512, 0, 1)
+        turn_y(1, 640, 0, 1)
+        store_words(1, 512, 256)
+        store_scales(1, [nc.scalar, nc.sync] * 2)

@@ -52,7 +52,7 @@ def tile_clipped_flux_reprojection_k4_kernel(
         gain_sb = kept("gain_sb", [P, DG, SLOTS], BF16)
         step_bf = kept("step_bf", [P, DG, SLOTS], BF16)
         step_sb = kept("step_sb", [P, DG, SLOTS], F32)
-        mix_raw = [kept("mix_raw%d" % h, [P, SLOTS, D], BF16) for h in range(DG)]
+        mix_raw = {0: kept("mix_raw", [P, SLOTS, D], BF16)}
         moves_raw = kept("moves_raw", [P, S // P, D], BF16)
         b_raw = [kept("b_raw%d" % g, [P, DG * 2 * PASS], U8) for g in range(RG)]
         b_codes = [kept("b_codes%d" % g, [P, SLOTS, DG * 2 * P], U8) for g in range(RG)]
@@ -91,8 +91,21 @@ def tile_clipped_flux_reprojection_k4_kernel(
                 in_=b_words[:, :, 2 * PASS * g : 2 * PASS * (g + 1)].bitcast(I32).rearrange("k p n -> p k n"),
             )
 
+        def load_z(s0, n):
+            nc.sync.dma_start(
+                out=z_codes[:, :, s0 : s0 + n].bitcast(I32),
+                in_=z_words.rearrange("k p n t -> p k (n t)").bitcast(I32)[:, :, s0 : s0 + n],
+            )
+
+        def load_vector(i, vec, queue):
+            queue.dma_start(out=vec_rows[RG * i : RG * (i + 1), :], in_=vec.rearrange("(g r) -> g r", g=RG))
+
         def mix_rows(h):
             return mix[PASS * h : PASS * (h + 1), :].rearrange("(p t) k -> p t k", t=SLOTS)
+
+        def load_late_mix():
+            mix_raw[1] = kept("mix_raw", [P, SLOTS, D], BF16)
+            nc.sync.dma_start(out=mix_raw[1][:], in_=mix_rows(1))
 
         def sort_b(g):
             nc.vector.tensor_copy(
@@ -122,16 +135,35 @@ def tile_clipped_flux_reprojection_k4_kernel(
                 nc.tensor.transpose(acc[:, t, :], vec_sorted[:, t, :], ident[:])
             nc.vector.tensor_copy(out=react[:], in_=acc[:, :, 0:16])
 
-        def turn_mix(h, t):
-            if t == 0:
+        def sort_words(dst, src):
+            nc.vector.tensor_copy(
+                out=dst.rearrange("p (k u c) -> p k u c", k=DG, u=2),
+                in_=src.bitcast(F32).rearrange("p (k c u) -> p k u c", k=DG, u=2),
+            )
+
+        def sort_mix(h, t):
+            words = work.tile([P, PASS], F32, name="sorted_words", bufs=6)
+            live["mix_words", h, t] = words
+            sort_words(words[:], mix_raw[h][:, t, :])
+
+        def sort_moves(j):
+            words = work.tile([P, PASS], F32, name="sorted_words", bufs=6)
+            live["moves_words", j] = words
+            sort_words(words[:], moves_raw[:, j, :])
+
+        def turn_mix(h, t, copy):
+            if h not in mix_grouped:
                 mix_grouped[h] = keep.tile([P, DG, SLOTS * PASS], BF16, name="mix_grouped", align_bytes=64)
             acc = bank([P, DG, 2, P])
-            words = mix_raw[h][:, t, :].bitcast(F32)
             for k in range(DG):
                 for u in range(2):
-                    nc.tensor.transpose(acc[:, k, u, :], words[:, 256 * k + u : 256 * (k + 1) : 2], ident[:])
+                    if ("mix_words", h, t) in live:
+                        src = live["mix_words", h, t][:, P * (2 * k + u) : P * (2 * k + u + 1)]
+                    else:
+                        src = mix_raw[h][:, t, :].bitcast(F32)[:, 256 * k + u : 256 * (k + 1) : 2]
+                    nc.tensor.transpose(acc[:, k, u, :], src, ident[:])
             dst = mix_grouped[h][:].bitcast(F32).rearrange("p k (c u) -> p k c u", u=2)
-            nc.scalar.copy(out=dst[:, :, P * t : P * (t + 1), :], in_=acc[:].rearrange("p k u c -> p k c u"))
+            copy(out=dst[:, :, P * t : P * (t + 1), :], in_=acc[:].rearrange("p k u c -> p k c u"))
 
         def quant_mix(h, k, c0, n):
             cols = slice(PASS * h + c0, PASS * h + c0 + n)
@@ -199,11 +231,20 @@ def tile_clipped_flux_reprojection_k4_kernel(
                         times_b(acc[:, e, c0 : c0 + P], g, 2 * pair + e, z_codes, z_sc,
                                 slice(S_MAIN + c0, S_MAIN + c0 + P))
 
+        def v_tail_copy(g):
+            rows = work.tile([P, SLOTS, S_TAIL], BF16, name="v_tail_raw", align_bytes=64)
+            live["v_tail_raw", g] = rows
+            for pair in range(2):
+                nc.scalar.copy(out=rows[:, 2 * pair : 2 * pair + 2, :], in_=live["v_tail_acc", g, pair][:])
+
         def v_tail_clip(g):
             rows = work.tile([P, SLOTS, S_TAIL], BF16, name="v_tail_rows", align_bytes=64)
             live["v_clipped", g, 1] = rows
             for t in range(SLOTS):
-                clip(rows[:, t, :], live["v_tail_acc", g, t // 2][:, t % 2, :], g, t)
+                if ("v_tail_raw", g) in live:
+                    clip(rows[:, t, :], live["v_tail_raw", g][:, t, :], g, t)
+                else:
+                    clip(rows[:, t, :], live["v_tail_acc", g, t // 2][:, t % 2, :], g, t)
 
         def v_main_clip(g):
             rows = work.tile([P, SLOTS, S_MAIN], BF16, name="v_main_rows", align_bytes=64)
@@ -232,8 +273,11 @@ def tile_clipped_flux_reprojection_k4_kernel(
                 )
 
         def turn_moves_into(dst, h, u, j):
-            words = moves_raw[:, j, :].bitcast(F32)
-            nc.tensor.transpose(dst, words[:, 256 * h + u : 256 * (h + 1) : 2], ident[:])
+            if ("moves_words", j) in live:
+                src = live["moves_words", j][:, P * (2 * h + u) : P * (2 * h + u + 1)]
+            else:
+                src = moves_raw[:, j, :].bitcast(F32)[:, 256 * h + u : 256 * (h + 1) : 2]
+            nc.tensor.transpose(dst, src, ident[:])
 
         def turn_moves_main(h, u):
             acc = bank([P, BANK])
@@ -250,7 +294,7 @@ def tile_clipped_flux_reprojection_k4_kernel(
                 scale_moves(h, u, S_MAIN, S_TAIL, acc[:, u, :])
 
         def p_product(h, s0, n, per_bank):
-            y_t = work.tile([P, SLOTS, n], F32, name="y_t", align_bytes=64, bufs=3)
+            y_t = work.tile([P, SLOTS, n], F32, name="y_t%d" % (n // BANK), align_bytes=64, bufs=3 - 2 * (n // BANK))
             live["y_t", h, s0] = y_t
             cols = slice(s0, s0 + n)
             for t0 in range(0, SLOTS, per_bank):
@@ -311,123 +355,145 @@ def tile_clipped_flux_reprojection_k4_kernel(
                 in_=rows[:],
             )
 
-        make_identity(nc, ident[:])
+        on_vector, on_scalar = nc.vector.tensor_copy, nc.scalar.copy
         nc.vector.memset(vec_rows[:], 0.0)
+        make_identity(nc, ident[:])
         nc.vector.memset(warm[:], 0.0)
         nc.vector.memset(bs_raw[0][:].bitcast(I32), 0)
-        nc.vector.memset(bs_raw[1][:].bitcast(I32), 0)
         nc.vector.memset(z_sc[:].rearrange("p k n -> p (k n)").bitcast(I32), 0)
+        nc.vector.memset(bs_raw[1][:].bitcast(I32), 0)
         nc.scalar.activation(out=warm[:, 0:1], in_=warm[:, 1:2], func=COPY, scale=warm[:, 2:3])
-        for t in range(SLOTS):
-            nc.sync.dma_start(out=mix_raw[0][:, t, :], in_=mix_rows(0)[:, t, :])
-        for i, vec in enumerate((react_weight, lower, upper)):
-            nc.sync.dma_start(out=vec_rows[RG * i : RG * (i + 1), :], in_=vec.rearrange("(g r) -> g r", g=RG))
+        load_vector(1, lower, nc.gpsimd)
+        load_vector(2, upper, nc.gpsimd)
+        nc.sync.dma_start(out=mix_raw[0][:, 0, :], in_=mix_rows(0)[:, 0, :])
+        nc.sync.dma_start(out=mix_raw[0][:, 1, :], in_=mix_rows(0)[:, 1, :])
+        nc.sync.dma_start(out=mix_raw[0][:, 2, :], in_=mix_rows(0)[:, 2, :])
+        nc.sync.dma_start(out=mix_raw[0][:, 3, :], in_=mix_rows(0)[:, 3, :])
+        load_vector(0, react_weight, nc.sync)
         load_b(0)
         load_b_scales(0)
-        load_b(1)
-        load_b_scales(1)
-        nc.sync.dma_start(out=z_codes[:].bitcast(I32), in_=z_words.rearrange("k p n t -> p k (n t)").bitcast(I32))
+        load_z(0, S)
         load_scales(z_sc[:], z_scales)
-        load_b(2)
-        nc.sync.dma_start(out=mix_raw[1][:], in_=mix_rows(1))
-        nc.sync.dma_start(out=gain_sb[:], in_=gain.rearrange("(h p t) -> p h t", h=DG, t=SLOTS))
-        nc.sync.dma_start(out=step_bf[:], in_=step.rearrange("(h p t) -> p h t", h=DG, t=SLOTS))
-        nc.sync.dma_start(out=moves_raw[:], in_=moves.rearrange("(j s) d -> s j d", s=P))
 
-        for t in range(SLOTS):
-            turn_mix(0, t)
-            if t == 2:
-                sort_vectors()
-            if t == 3:
-                sort_b(0)
-                sort_b_scales(0)
-            for k in range(DG):
-                quant_mix(0, k, P * t, P)
+        turn_mix(0, 0, on_scalar)
+        sort_vectors()
+        turn_mix(0, 1, on_scalar)
+        turn_mix(0, 2, on_scalar)
+        turn_mix(0, 3, on_scalar)
+        sort_b(0)
+        quant_mix(0, 0, 2 * P, P)
+        sort_b_scales(0)
+        quant_mix(0, 0, 0, 2 * P)
+        quant_mix(0, 0, 3 * P, P)
+        quant_mix(0, 1, 2 * P, P)
+        load_late_mix()
+        nc.sync.dma_start(out=step_bf[:], in_=step.rearrange("(h p t) -> p h t", h=DG, t=SLOTS))
+        load_b(1)
+        nc.sync.dma_start(out=gain_sb[:], in_=gain.rearrange("(h p t) -> p h t", h=DG, t=SLOTS))
+        quant_mix(0, 1, 0, 2 * P)
+        quant_mix(0, 1, 3 * P, P)
         turn_vectors()
+        sort_mix(1, 1)
         q_product(0, 0)
-        sort_b(1)
-        sort_b_scales(1)
-        q_product(0, 1)
-        q_group(0, 0)
-        sort_b(2)
-        q_quant(0, 0)
+        sort_mix(1, 3)
         v_main(0)
-        q_group(0, 1)
         v_tail(0)
-        nc.vector.tensor_copy(out=step_sb[:], in_=step_bf[:])
-        q_quant(0, 1)
-        v_main_clip(0)
-        v_tail_clip(0)
-        for t in range(SLOTS):
-            turn_mix(1, t)
-        v_group(0, 0)
-        v_group(0, 1)
-        v_quant(0, 0)
-        v_quant(0, 1)
-        q_product(0, 2)
-        for k in range(DG):
-            quant_mix(1, k, 0, PASS)
+        load_b_scales(1)
+        sort_mix(1, 2)
+        v_tail_copy(0)
+        sort_b(1)
+        q_group(0, 0)
+        sort_b_scales(1)
         v_main(1)
-        q_group(0, 2)
+        v_main_clip(0)
+        sort_mix(1, 0)
+        v_group(0, 0)
+        load_b(2)
+        v_tail_clip(0)
+        nc.sync.dma_start(out=moves_raw[:], in_=moves.rearrange("(j s) d -> s j d", s=P))
         v_tail(1)
+        v_quant(0, 0)
+        sort_b(2)
         v_main_clip(1)
-        q_quant(0, 2)
+        nc.vector.tensor_copy(out=step_sb[:], in_=step_bf[:])
+        v_tail_copy(1)
+        sort_moves(1)
+        v_group(0, 1)
         v_tail_clip(1)
-        q_product(1, 0)
-        v_group(1, 0)
         v_group(1, 1)
-        v_quant(1, 0)
-        v_quant(1, 1)
+        sort_moves(5)
+        q_quant(0, 0)
+        turn_mix(1, 0, on_scalar)
+        turn_mix(1, 1, on_scalar)
+        v_group(1, 0)
+        turn_mix(1, 2, on_scalar)
+        turn_mix(1, 3, on_scalar)
+        sort_moves(0)
+        quant_mix(1, 1, 0, PASS)
+        quant_mix(1, 0, 0, PASS)
         v_main(2)
-        q_group(1, 0)
         v_tail(2)
         v_main_clip(2)
-        q_quant(1, 0)
+        sort_moves(3)
+        v_group(2, 0)
+        sort_moves(2)
+        v_quant(1, 0)
+        v_tail_copy(2)
+        q_product(0, 1)
+        v_quant(1, 1)
+        q_group(0, 1)
+        q_product(0, 2)
+        sort_moves(4)
+        q_group(0, 2)
+        v_quant(2, 0)
+        q_product(1, 0)
+        v_quant(0, 1)
         v_tail_clip(2)
+        q_quant(0, 2)
+        q_quant(0, 1)
+        q_product(1, 1)
         turn_moves_main(0, 0)
+        v_group(2, 1)
         turn_moves_main(0, 1)
         turn_moves_tail(0)
-        v_group(2, 0)
-        v_group(2, 1)
-        v_quant(2, 0)
-        v_quant(2, 1)
-        on_vector, on_scalar = nc.vector.tensor_copy, nc.scalar.copy
-        q_product(1, 1)
-        p_product(0, 0, 512, 1)
-        q_product(1, 2)
+        q_group(1, 0)
         q_group(1, 1)
+        q_product(1, 2)
+        v_quant(2, 1)
+        q_quant(1, 1)
+        q_quant(1, 0)
+        p_product(0, 0, 512, 1)
         turn_moves_main(1, 0)
         turn_moves_main(1, 1)
-        q_quant(1, 1)
+        turn_moves_tail(1)
         q_group(1, 2)
         p_product(0, 512, 256, 2)
         q_quant(1, 2)
-        turn_y(0, 0, 0, 2)
-        turn_moves_tail(1)
         y_group(0, 0, 512, on_vector)
+        y_group(0, 512, 256, on_vector)
+        turn_y(0, 0, 0, 2)
         turn_y(0, 0, 2, 2)
         p_product(1, 0, 256, 2)
         y_quant(0, 0, 512)
-        y_group(0, 512, 256, on_vector)
         turn_y(0, 512, 0, 2)
-        p_product(1, 256, 256, 2)
+        y_group(1, 0, 256, on_scalar)
         y_quant(0, 512, 256)
         store_words(0, 0, 768)
-        store_scales(0, [nc.sync] * 4)
-        y_group(1, 0, 256, on_scalar)
-        turn_y(1, 0, 0, 2)
-        p_product(1, 512, 128, 4)
-        y_quant(1, 0, 256)
+        p_product(1, 256, 256, 2)
         y_group(1, 256, 256, on_vector)
-        turn_y(1, 256, 0, 2)
-        p_product(1, 640, 128, 1)
+        y_quant(1, 0, 256)
+        turn_y(1, 0, 0, 2)
         y_quant(1, 256, 256)
         store_words(1, 0, 512)
+        store_scales(0, [nc.sync] * 4)
+        p_product(1, 512, 128, 4)
+        turn_y(1, 256, 0, 2)
+        p_product(1, 640, 128, 1)
         y_group(1, 512, 128, on_vector)
         y_group(1, 640, 128, on_vector)
         y_quant(1, 512, 128)
-        y_quant(1, 640, 128)
         turn_y(1, 512, 0, 1)
-        turn_y(1, 640, 0, 1)
+        y_quant(1, 640, 128)
         store_words(1, 512, 256)
+        turn_y(1, 640, 0, 1)
         store_scales(1, [nc.scalar, nc.sync] * 2)

@@ -25,6 +25,11 @@ BANK = 512
 S_MAIN = 512
 S_TAIL = S - S_MAIN
 B_SCALE_PARTS = ((0, 1), (1, 2))
+MIX_COL = (PASS, 0)
+Z_COL = D
+HALF = PASS // 2
+MOVING = D + S
+QF = 2
 
 
 def tile_clipped_flux_reprojection_k4_kernel(
@@ -48,7 +53,7 @@ def tile_clipped_flux_reprojection_k4_kernel(
         warm = kept("warm", [P, 8], F32)
         vec_rows = kept("vec_rows", [P, PASS], BF16)
         vec_sorted = kept("vec_sorted", [P, SLOTS, P], F32)
-        react = kept("react", [P, SLOTS, 16], F32)
+        react = kept("react", [P, 16, SLOTS], F32)
         gain_sb = kept("gain_sb", [P, DG, SLOTS], BF16)
         step_bf = kept("step_bf", [P, DG, SLOTS], BF16)
         step_sb = kept("step_sb", [P, DG, SLOTS], F32)
@@ -58,10 +63,8 @@ def tile_clipped_flux_reprojection_k4_kernel(
         b_codes = [kept("b_codes%d" % g, [P, SLOTS, DG * 2 * P], U8) for g in range(RG)]
         bs_raw = [kept("bs_raw%d" % i, [P, DG * PASS * n], U8) for i, (g0, n) in enumerate(B_SCALE_PARTS)]
         b_sc = [kept("b_sc%d" % i, [P, SLOTS, DG * P * n], U8) for i, (g0, n) in enumerate(B_SCALE_PARTS)]
-        z_codes = kept("z_codes", [P, DG, S], U32)
-        z_sc = kept("z_sc", [P, DG, S], U8)
-        mix_codes = kept("mix_codes", [P, DG, D], U32)
-        mix_sc = kept("mix_sc", [P, DG, D], U8)
+        mov_codes = kept("mov_codes", [P, DG, MOVING], U32)
+        mov_sc = kept("mov_sc", [P, DG, MOVING], U8)
         q_codes = kept("q_codes", [P, RG, D], U32)
         q_sc = kept("q_sc", [P, RG, D], U8)
         v_codes = kept("v_codes", [P, RG, S], U32)
@@ -93,7 +96,7 @@ def tile_clipped_flux_reprojection_k4_kernel(
 
         def load_z(s0, n):
             nc.sync.dma_start(
-                out=z_codes[:, :, s0 : s0 + n].bitcast(I32),
+                out=mov_codes[:, :, Z_COL + s0 : Z_COL + s0 + n].bitcast(I32),
                 in_=z_words.rearrange("k p n t -> p k (n t)").bitcast(I32)[:, :, s0 : s0 + n],
             )
 
@@ -133,23 +136,23 @@ def tile_clipped_flux_reprojection_k4_kernel(
             acc = bank([P, SLOTS, P])
             for t in range(SLOTS):
                 nc.tensor.transpose(acc[:, t, :], vec_sorted[:, t, :], ident[:])
-            nc.vector.tensor_copy(out=react[:], in_=acc[:, :, 0:16])
+            nc.vector.tensor_copy(out=react[:], in_=acc[:, :, 0:16].rearrange("p t r -> p r t"))
 
-        def sort_words(dst, src):
-            nc.vector.tensor_copy(
+        def sort_words(dst, src, copy):
+            copy(
                 out=dst.rearrange("p (k u c) -> p k u c", k=DG, u=2),
                 in_=src.bitcast(F32).rearrange("p (k c u) -> p k u c", k=DG, u=2),
             )
 
-        def sort_mix(h, t):
+        def sort_mix(h, t, copy=nc.vector.tensor_copy):
             words = work.tile([P, PASS], F32, name="sorted_words", bufs=6)
             live["mix_words", h, t] = words
-            sort_words(words[:], mix_raw[h][:, t, :])
+            sort_words(words[:], mix_raw[h][:, t, :], copy)
 
-        def sort_moves(j):
+        def sort_moves(j, copy=nc.vector.tensor_copy):
             words = work.tile([P, PASS], F32, name="sorted_words", bufs=6)
             live["moves_words", j] = words
-            sort_words(words[:], moves_raw[:, j, :])
+            sort_words(words[:], moves_raw[:, j, :], copy)
 
         def turn_mix(h, t, copy):
             if h not in mix_grouped:
@@ -166,14 +169,14 @@ def tile_clipped_flux_reprojection_k4_kernel(
             copy(out=dst[:, :, P * t : P * (t + 1), :], in_=acc[:].rearrange("p k u c -> p k c u"))
 
         def quant_mix(h, k, c0, n):
-            cols = slice(PASS * h + c0, PASS * h + c0 + n)
+            cols = slice(MIX_COL[h] + c0, MIX_COL[h] + c0 + n)
             nc.vector.quantize_mx(
-                out=mix_codes[:, k, cols].bitcast(FP8X4),
-                scales=mix_sc[:, k, cols],
+                out=mov_codes[:, k, cols].bitcast(FP8X4),
+                scales=mov_sc[:, k, cols],
                 in_=mix_grouped[h][:, k, SLOTS * c0 : SLOTS * (c0 + n)],
             )
 
-        def times_b(dst, g, t, codes, scales, cols):
+        def times_b(dst, g, t, cols):
             part = min(g, 1)
             g0, n = B_SCALE_PARTS[part]
             for k in range(DG):
@@ -182,24 +185,72 @@ def tile_clipped_flux_reprojection_k4_kernel(
                     out=dst,
                     lhsT=b_codes[g][:, t, 2 * P * k : 2 * P * (k + 1)].bitcast(FP4X4),
                     lhsT_scale=b_sc[part][:, t, P * m : P * (m + 1)],
-                    rhs=codes[:, k, cols].bitcast(FP8X4),
-                    rhs_scale=scales[:, k, cols],
+                    rhs=mov_codes[:, k, cols].bitcast(FP8X4),
+                    rhs_scale=mov_sc[:, k, cols],
                     start=(k == 0),
                     stop=(k == DG - 1),
                 )
 
-        def q_product(h, g):
-            rows = work.tile([P, SLOTS, PASS], BF16, name="q_rows", align_bytes=64)
-            live["q_rows", h, g] = rows
+        def weigh(dst, src, g, t):
+            nc.scalar.activation(out=dst, in_=src, func=COPY, scale=react[:, g, t : t + 1])
+
+        def q_narrow_mm(g, c):
+            acc = bank([P, SLOTS, P])
+            live["q_narrow", g, c] = acc
+            c0 = MIX_COL[0] + P * c
+            for t in range(SLOTS):
+                times_b(acc[:, t, :], g, t, slice(c0, c0 + P))
+
+        def q_narrow_out(g, c):
+            if ("q_grouped", 0, g) not in live:
+                live["q_grouped", 0, g] = work.tile([P, SLOTS * PASS], BF16, name="q_grouped", align_bytes=64, bufs=3)
+            acc = live["q_narrow", g, c]
+            nc.vector.tensor_tensor(
+                out=live["q_grouped", 0, g][:, BANK * c : BANK * (c + 1)].rearrange("p (n t) -> p n t", t=SLOTS),
+                in0=acc[:].rearrange("p t n -> p n t"),
+                in1=react[:, g : g + 1, :].to_broadcast([P, P, SLOTS]),
+                op=ALU.mult,
+            )
+
+        def v_rows_of(g):
+            if ("v_rows", g) not in live:
+                live["v_rows", g] = work.tile([P, SLOTS, S], BF16, name="v_rows", align_bytes=64)
+            return live["v_rows", g]
+
+        def shared_product(g):
+            q_rows = work.tile([P, SLOTS, HALF], BF16, name="q_half_rows", align_bytes=64)
+            v_rows = v_rows_of(g)
+            live["q_rows", 0, g] = q_rows
             for t in range(SLOTS):
                 acc = bank([P, BANK])
-                times_b(acc[:], g, t, mix_codes, mix_sc, slice(PASS * h, PASS * (h + 1)))
-                nc.scalar.activation(out=rows[:, t, :], in_=acc[:], func=COPY, scale=react[:, t, g : g + 1])
+                times_b(acc[:], g, t, slice(Z_COL - HALF, Z_COL + HALF))
+                weigh(q_rows[:, t, :], acc[:, :HALF], g, t)
+                nc.scalar.copy(out=v_rows[:, t, :HALF], in_=acc[:, HALF:])
+
+        def v_product(g):
+            v_rows = v_rows_of(g)
+            for t in range(SLOTS):
+                acc = bank([P, BANK])
+                times_b(acc[:], g, t, slice(Z_COL + HALF, MOVING))
+                nc.scalar.copy(out=v_rows[:, t, HALF:], in_=acc[:])
+
+        def q_product(g):
+            rows = work.tile([P, SLOTS, PASS], BF16, name="q_rows", align_bytes=64)
+            live["q_rows", 1, g] = rows
+            for t in range(SLOTS):
+                acc = bank([P, BANK])
+                times_b(acc[:], g, t, slice(MIX_COL[1], MIX_COL[1] + PASS))
+                weigh(rows[:, t, :], acc[:], g, t)
 
         def q_group(h, g):
-            grouped = work.tile([P, SLOTS * PASS], BF16, name="q_grouped", align_bytes=64)
-            live["q_grouped", h, g] = grouped
-            interleave(grouped[:], live["q_rows", h, g][:])
+            if h == 0:
+                if ("q_grouped", 0, g) not in live:
+                    live["q_grouped", 0, g] = work.tile([P, SLOTS * PASS], BF16, name="q_grouped", align_bytes=64, bufs=3)
+                interleave(live["q_grouped", 0, g][:, SLOTS * HALF :], live["q_rows", 0, g][:])
+            else:
+                grouped = work.tile([P, SLOTS * PASS], BF16, name="q_grouped", align_bytes=64, bufs=3)
+                live["q_grouped", 1, g] = grouped
+                interleave(grouped[:], live["q_rows", 1, g][:])
 
         def q_quant(h, g):
             cols = slice(PASS * h, PASS * (h + 1))
@@ -207,62 +258,27 @@ def tile_clipped_flux_reprojection_k4_kernel(
                 out=q_codes[:, g, cols].bitcast(FP8X4), scales=q_sc[:, g, cols], in_=live["q_grouped", h, g][:]
             )
 
-        def clip(dst, src, g, t):
-            nc.vector.tensor_scalar(
-                out=dst, in0=src,
-                scalar1=react[:, t, RG + g : RG + g + 1], scalar2=react[:, t, 2 * RG + g : 2 * RG + g + 1],
-                op0=ALU.max, op1=ALU.min,
-            )
-
-        def v_main(g):
-            rows = work.tile([P, SLOTS, S_MAIN], BF16, name="v_rows", align_bytes=64)
-            live["v_rows", g] = rows
+        def v_clip(g):
+            rows = work.tile([P, SLOTS, S], BF16, name="v_clipped", align_bytes=64)
+            live["v_clipped", g] = rows
             for t in range(SLOTS):
-                acc = bank([P, BANK])
-                times_b(acc[:], g, t, z_codes, z_sc, slice(0, S_MAIN))
-                nc.scalar.copy(out=rows[:, t, :], in_=acc[:])
+                nc.vector.tensor_scalar(
+                    out=rows[:, t, :], in0=live["v_rows", g][:, t, :],
+                    scalar1=react[:, RG + g, t : t + 1], scalar2=react[:, 2 * RG + g, t : t + 1],
+                    op0=ALU.max, op1=ALU.min,
+                )
 
-        def v_tail(g):
-            for pair in range(2):
-                acc = bank([P, 2, S_TAIL])
-                live["v_tail_acc", g, pair] = acc
-                for e in range(2):
-                    for c0 in range(0, S_TAIL, P):
-                        times_b(acc[:, e, c0 : c0 + P], g, 2 * pair + e, z_codes, z_sc,
-                                slice(S_MAIN + c0, S_MAIN + c0 + P))
+        def v_group(g):
+            grouped = work.tile([P, SLOTS * S], BF16, name="v_grouped", align_bytes=64)
+            live["v_grouped", g] = grouped
+            interleave(grouped[:], live["v_clipped", g][:])
 
-        def v_tail_copy(g):
-            rows = work.tile([P, SLOTS, S_TAIL], BF16, name="v_tail_raw", align_bytes=64)
-            live["v_tail_raw", g] = rows
-            for pair in range(2):
-                nc.scalar.copy(out=rows[:, 2 * pair : 2 * pair + 2, :], in_=live["v_tail_acc", g, pair][:])
-
-        def v_tail_clip(g):
-            rows = work.tile([P, SLOTS, S_TAIL], BF16, name="v_tail_rows", align_bytes=64)
-            live["v_clipped", g, 1] = rows
-            for t in range(SLOTS):
-                if ("v_tail_raw", g) in live:
-                    clip(rows[:, t, :], live["v_tail_raw", g][:, t, :], g, t)
-                else:
-                    clip(rows[:, t, :], live["v_tail_acc", g, t // 2][:, t % 2, :], g, t)
-
-        def v_main_clip(g):
-            rows = work.tile([P, SLOTS, S_MAIN], BF16, name="v_main_rows", align_bytes=64)
-            live["v_clipped", g, 0] = rows
-            for t in range(SLOTS):
-                clip(rows[:, t, :], live["v_rows", g][:, t, :], g, t)
-
-        def v_group(g, part):
-            n = (S_MAIN, S_TAIL)[part]
-            grouped = work.tile([P, SLOTS * n], BF16, name="v_grouped%d" % part, align_bytes=64)
-            live["v_grouped", g, part] = grouped
-            interleave(grouped[:], live["v_clipped", g, part][:])
-
-        def v_quant(g, part):
-            cols = (slice(0, S_MAIN), slice(S_MAIN, S))[part]
-            nc.vector.quantize_mx(
-                out=v_codes[:, g, cols].bitcast(FP8X4), scales=v_sc[:, g, cols], in_=live["v_grouped", g, part][:]
-            )
+        def v_quant(g):
+            for c0, c1 in ((0, HALF), (HALF, S)):
+                nc.vector.quantize_mx(
+                    out=v_codes[:, g, c0:c1].bitcast(FP8X4), scales=v_sc[:, g, c0:c1],
+                    in_=live["v_grouped", g][:, SLOTS * c0 : SLOTS * c1],
+                )
 
         def scale_moves(h, u, s0, n, acc):
             pairs = acc.bitcast(BF16).rearrange("p (s e) -> p e s", e=2)
@@ -339,160 +355,152 @@ def tile_clipped_flux_reprojection_k4_kernel(
                     in_=y_sc[32 * q : 32 * q + 4, h, :].bitcast(I32),
                 )
 
-        def turn_y(h, s0, j0, count):
-            rows = work.tile([P, count, PASS], F32, name="y_rows", align_bytes=64, bufs=3)
-            for j in range(count):
+        def turn_y(h, s0, j0, count, copy=nc.scalar.copy):
+            for j in range(j0, j0 + count):
+                rows = work.tile([P, PASS], F32, name="y_rows", align_bytes=64, bufs=6)
                 acc = bank([P, SLOTS, P])
                 for t in range(SLOTS):
-                    c0 = P * (j0 + j)
-                    nc.tensor.transpose(acc[:, t, :], live["y_t", h, s0][:, t, c0 : c0 + P], ident[:])
-                nc.scalar.copy(
-                    out=rows[:, j, :].rearrange("s (p t) -> s p t", t=SLOTS), in_=acc[:].rearrange("s t p -> s p t")
-                )
-            r0 = s0 + P * j0
-            nc.sync.dma_start(
-                out=out_0[r0 : r0 + P * count, PASS * h : PASS * (h + 1)].rearrange("(j s) d -> s j d", s=P),
-                in_=rows[:],
-            )
+                    nc.tensor.transpose(acc[:, t, :], live["y_t", h, s0][:, t, P * j : P * (j + 1)], ident[:])
+                copy(out=rows[:].rearrange("s (p t) -> s p t", t=SLOTS), in_=acc[:].rearrange("s t p -> s p t"))
+                r0 = s0 + P * j
+                nc.sync.dma_start(out=out_0[r0 : r0 + P, PASS * h : PASS * (h + 1)], in_=rows[:])
 
         on_vector, on_scalar = nc.vector.tensor_copy, nc.scalar.copy
         nc.vector.memset(vec_rows[:], 0.0)
         make_identity(nc, ident[:])
         nc.vector.memset(warm[:], 0.0)
         nc.vector.memset(bs_raw[0][:].bitcast(I32), 0)
-        nc.vector.memset(z_sc[:].rearrange("p k n -> p (k n)").bitcast(I32), 0)
+        nc.vector.memset(mov_sc[:, :, Z_COL:].bitcast(I32), 0)
         nc.vector.memset(bs_raw[1][:].bitcast(I32), 0)
         nc.scalar.activation(out=warm[:, 0:1], in_=warm[:, 1:2], func=COPY, scale=warm[:, 2:3])
+        load_vector(0, react_weight, nc.gpsimd)
         load_vector(1, lower, nc.gpsimd)
         load_vector(2, upper, nc.gpsimd)
         nc.sync.dma_start(out=mix_raw[0][:, 0, :], in_=mix_rows(0)[:, 0, :])
         nc.sync.dma_start(out=mix_raw[0][:, 1, :], in_=mix_rows(0)[:, 1, :])
-        nc.sync.dma_start(out=mix_raw[0][:, 2, :], in_=mix_rows(0)[:, 2, :])
-        nc.sync.dma_start(out=mix_raw[0][:, 3, :], in_=mix_rows(0)[:, 3, :])
-        load_vector(0, react_weight, nc.sync)
         load_b(0)
         load_b_scales(0)
+        nc.sync.dma_start(out=mix_raw[0][:, 2, :], in_=mix_rows(0)[:, 2, :])
+        nc.sync.dma_start(out=mix_raw[0][:, 3, :], in_=mix_rows(0)[:, 3, :])
         load_z(0, S)
-        load_scales(z_sc[:], z_scales)
+        load_scales(mov_sc[:, :, Z_COL:], z_scales)
 
         turn_mix(0, 0, on_scalar)
-        sort_vectors()
+        sort_mix(0, 1)
         turn_mix(0, 1, on_scalar)
+        sort_b_scales(0)
+        sort_b(0)
+        quant_mix(0, 0, 0, P)
+        quant_mix(0, 1, 0, P)
+        q_narrow_mm(0, 0)
+        quant_mix(0, 0, P, P)
+        quant_mix(0, 1, P, P)
+        q_narrow_mm(0, 1)
+        sort_mix(0, 2)
+        sort_mix(0, 3)
+        sort_vectors()
         turn_mix(0, 2, on_scalar)
         turn_mix(0, 3, on_scalar)
-        sort_b(0)
-        quant_mix(0, 0, 2 * P, P)
-        sort_b_scales(0)
-        quant_mix(0, 0, 0, 2 * P)
-        quant_mix(0, 0, 3 * P, P)
-        quant_mix(0, 1, 2 * P, P)
+        load_b(1)
+        load_b_scales(1)
+        load_b(2)
         load_late_mix()
         nc.sync.dma_start(out=step_bf[:], in_=step.rearrange("(h p t) -> p h t", h=DG, t=SLOTS))
-        load_b(1)
         nc.sync.dma_start(out=gain_sb[:], in_=gain.rearrange("(h p t) -> p h t", h=DG, t=SLOTS))
-        quant_mix(0, 1, 0, 2 * P)
-        quant_mix(0, 1, 3 * P, P)
-        turn_vectors()
-        sort_mix(1, 1)
-        q_product(0, 0)
-        sort_mix(1, 3)
-        v_main(0)
-        v_tail(0)
-        load_b_scales(1)
-        sort_mix(1, 2)
-        v_tail_copy(0)
-        sort_b(1)
-        q_group(0, 0)
-        sort_b_scales(1)
-        v_main(1)
-        v_main_clip(0)
-        sort_mix(1, 0)
-        v_group(0, 0)
-        load_b(2)
-        v_tail_clip(0)
         nc.sync.dma_start(out=moves_raw[:], in_=moves.rearrange("(j s) d -> s j d", s=P))
-        v_tail(1)
-        v_quant(0, 0)
+        sort_b(1)
+        turn_vectors()
+        q_narrow_out(0, 0)
+        q_narrow_out(0, 1)
+        quant_mix(0, 0, 2 * P, 2 * P)
+        quant_mix(0, 1, 2 * P, 2 * P)
+        v_product(0)
+        sort_b_scales(1)
         sort_b(2)
-        v_main_clip(1)
-        nc.vector.tensor_copy(out=step_sb[:], in_=step_bf[:])
-        v_tail_copy(1)
+        sort_mix(1, 0)
+        sort_mix(1, 1)
+        shared_product(0)
+        v_clip(0)
+        q_narrow_mm(1, 0)
+        q_narrow_mm(1, 1)
+        q_narrow_out(1, 0)
+        q_narrow_out(1, 1)
+        v_group(0)
+        v_product(1)
+        shared_product(1)
+        q_group(0, 0)
+        q_narrow_mm(2, 0)
+        q_narrow_mm(2, 1)
+        sort_mix(1, 2, on_scalar)
+        sort_mix(1, 3, on_scalar)
+        sort_moves(0)
+        v_quant(0)
         sort_moves(1)
-        v_group(0, 1)
-        v_tail_clip(1)
-        v_group(1, 1)
-        sort_moves(5)
-        q_quant(0, 0)
+        v_clip(1)
+        q_narrow_out(2, 0)
+        q_narrow_out(2, 1)
         turn_mix(1, 0, on_scalar)
         turn_mix(1, 1, on_scalar)
-        v_group(1, 0)
         turn_mix(1, 2, on_scalar)
         turn_mix(1, 3, on_scalar)
-        sort_moves(0)
-        quant_mix(1, 1, 0, PASS)
-        quant_mix(1, 0, 0, PASS)
-        v_main(2)
-        v_tail(2)
-        v_main_clip(2)
-        sort_moves(3)
-        v_group(2, 0)
-        sort_moves(2)
-        v_quant(1, 0)
-        v_tail_copy(2)
-        q_product(0, 1)
-        v_quant(1, 1)
         q_group(0, 1)
-        q_product(0, 2)
-        sort_moves(4)
-        q_group(0, 2)
-        v_quant(2, 0)
-        q_product(1, 0)
-        v_quant(0, 1)
-        v_tail_clip(2)
-        q_quant(0, 2)
+        q_quant(0, 0)
         q_quant(0, 1)
-        q_product(1, 1)
+        v_product(2)
+        sort_moves(2)
+        sort_moves(3)
+        quant_mix(1, 0, 0, PASS)
+        quant_mix(1, 1, 0, PASS)
+        v_group(1)
+        shared_product(2)
+        q_product(0)
+        v_clip(2)
+        q_group(0, 2)
+        v_quant(1)
+        v_group(2)
+        nc.vector.tensor_copy(out=step_sb[:], in_=step_bf[:])
+        q_group(1, 0)
+        v_quant(2)
+        q_quant(0, 2)
+        q_product(1)
         turn_moves_main(0, 0)
-        v_group(2, 1)
         turn_moves_main(0, 1)
         turn_moves_tail(0)
-        q_group(1, 0)
-        q_group(1, 1)
-        q_product(1, 2)
-        v_quant(2, 1)
-        q_quant(1, 1)
         q_quant(1, 0)
+        q_group(1, 1)
+        q_product(2)
         p_product(0, 0, 512, 1)
+        q_group(1, 2)
+        q_quant(1, 1)
+        q_quant(1, 2)
         turn_moves_main(1, 0)
         turn_moves_main(1, 1)
         turn_moves_tail(1)
-        q_group(1, 2)
         p_product(0, 512, 256, 2)
-        q_quant(1, 2)
-        y_group(0, 0, 512, on_vector)
-        y_group(0, 512, 256, on_vector)
         turn_y(0, 0, 0, 2)
         turn_y(0, 0, 2, 2)
+        y_group(0, 0, 512, on_vector)
+        y_group(0, 512, 256, on_scalar)
         p_product(1, 0, 256, 2)
         y_quant(0, 0, 512)
         turn_y(0, 512, 0, 2)
-        y_group(1, 0, 256, on_scalar)
         y_quant(0, 512, 256)
         store_words(0, 0, 768)
+        store_scales(0, [nc.sync] * 4)
         p_product(1, 256, 256, 2)
+        y_group(1, 0, 256, on_scalar)
         y_group(1, 256, 256, on_vector)
         y_quant(1, 0, 256)
         turn_y(1, 0, 0, 2)
         y_quant(1, 256, 256)
         store_words(1, 0, 512)
-        store_scales(0, [nc.sync] * 4)
         p_product(1, 512, 128, 4)
         turn_y(1, 256, 0, 2)
         p_product(1, 640, 128, 1)
         y_group(1, 512, 128, on_vector)
         y_group(1, 640, 128, on_vector)
-        y_quant(1, 512, 128)
         turn_y(1, 512, 0, 1)
+        y_quant(1, 512, 128)
         y_quant(1, 640, 128)
         store_words(1, 512, 256)
         turn_y(1, 640, 0, 1)

@@ -380,126 +380,128 @@ def tile_clipped_flux_reprojection_k4_kernel(
         nc.sync.dma_start(out=mix_raw[0][:, 1, :], in_=mix_rows(0)[:, 1, :])
         load_b(0)
         load_b_scales(0)
+        load_scales(mov_sc[:, :, Z_COL:], z_scales)
         nc.sync.dma_start(out=mix_raw[0][:, 2, :], in_=mix_rows(0)[:, 2, :])
         nc.sync.dma_start(out=mix_raw[0][:, 3, :], in_=mix_rows(0)[:, 3, :])
         load_z(0, S)
-        load_scales(mov_sc[:, :, Z_COL:], z_scales)
 
         turn_mix(0, 0, on_scalar)
         sort_mix(0, 1)
         turn_mix(0, 1, on_scalar)
-        sort_b_scales(0)
         sort_b(0)
+        sort_b_scales(0)
         quant_mix(0, 0, 0, P)
         quant_mix(0, 1, 0, P)
-        q_narrow_mm(0, 0)
+        sort_vectors()
         quant_mix(0, 0, P, P)
         quant_mix(0, 1, P, P)
-        q_narrow_mm(0, 1)
+        q_narrow_mm(0, 0)
         sort_mix(0, 2)
         sort_mix(0, 3)
-        sort_vectors()
         turn_mix(0, 2, on_scalar)
         turn_mix(0, 3, on_scalar)
-        load_b(1)
         load_b_scales(1)
+        load_b(1)
         load_b(2)
         load_late_mix()
         nc.sync.dma_start(out=step_bf[:], in_=step.rearrange("(h p t) -> p h t", h=DG, t=SLOTS))
         nc.sync.dma_start(out=gain_sb[:], in_=gain.rearrange("(h p t) -> p h t", h=DG, t=SLOTS))
         nc.sync.dma_start(out=moves_raw[:], in_=moves.rearrange("(j s) d -> s j d", s=P))
-        sort_b(1)
         turn_vectors()
         q_narrow_out(0, 0)
+        q_narrow_mm(0, 1)
+        v_product(0)
         q_narrow_out(0, 1)
         quant_mix(0, 0, 2 * P, 2 * P)
         quant_mix(0, 1, 2 * P, 2 * P)
-        v_product(0)
-        sort_b_scales(1)
+        sort_b(1)
         sort_b(2)
-        sort_mix(1, 0)
-        sort_mix(1, 1)
+        sort_b_scales(1)
         shared_product(0)
-        v_clip(0)
-        q_narrow_mm(1, 0)
-        q_narrow_mm(1, 1)
-        q_narrow_out(1, 0)
-        q_narrow_out(1, 1)
-        v_group(0)
-        v_product(1)
-        shared_product(1)
-        q_group(0, 0)
-        q_narrow_mm(2, 0)
-        q_narrow_mm(2, 1)
         sort_mix(1, 2, on_scalar)
         sort_mix(1, 3, on_scalar)
-        sort_moves(0)
-        v_quant(0)
-        sort_moves(1)
-        v_clip(1)
-        q_narrow_out(2, 0)
-        q_narrow_out(2, 1)
+        sort_mix(1, 0)
+        sort_mix(1, 1)
+        nc.vector.tensor_copy(out=step_sb[:], in_=step_bf[:])
+        q_narrow_mm(1, 0)
+        q_narrow_mm(1, 1)
+        shared_product(1)
+        v_clip(0)
+        q_narrow_out(1, 0)
+        q_narrow_out(1, 1)
+        q_group(0, 0)
+        v_product(1)
+        v_group(0)
         turn_mix(1, 0, on_scalar)
         turn_mix(1, 1, on_scalar)
         turn_mix(1, 2, on_scalar)
         turn_mix(1, 3, on_scalar)
+        sort_moves(0)
+        sort_moves(1)
+        v_quant(0)
+        v_clip(1)
         q_group(0, 1)
         q_quant(0, 0)
-        q_quant(0, 1)
-        v_product(2)
+        q_narrow_mm(2, 0)
+        q_narrow_mm(2, 1)
         sort_moves(2)
         sort_moves(3)
+        q_narrow_out(2, 0)
         quant_mix(1, 0, 0, PASS)
         quant_mix(1, 1, 0, PASS)
+        sort_moves(4)
+        sort_moves(5)
+        q_narrow_out(2, 1)
         v_group(1)
         shared_product(2)
-        q_product(0)
+        v_product(2)
         v_clip(2)
         q_group(0, 2)
+        q_quant(0, 1)
         v_quant(1)
         v_group(2)
-        nc.vector.tensor_copy(out=step_sb[:], in_=step_bf[:])
-        q_group(1, 0)
-        v_quant(2)
+        q_product(0)
         q_quant(0, 2)
+        v_quant(2)
         q_product(1)
         turn_moves_main(0, 0)
         turn_moves_main(0, 1)
         turn_moves_tail(0)
-        q_quant(1, 0)
+        q_group(1, 0)
         q_group(1, 1)
         q_product(2)
         p_product(0, 0, 512, 1)
-        q_group(1, 2)
-        q_quant(1, 1)
-        q_quant(1, 2)
         turn_moves_main(1, 0)
         turn_moves_main(1, 1)
         turn_moves_tail(1)
-        p_product(0, 512, 256, 2)
         turn_y(0, 0, 0, 2)
         turn_y(0, 0, 2, 2)
+        q_group(1, 2)
+        q_quant(1, 0)
+        q_quant(1, 1)
+        q_quant(1, 2)
+        p_product(0, 512, 256, 2)
         y_group(0, 0, 512, on_vector)
-        y_group(0, 512, 256, on_scalar)
         p_product(1, 0, 256, 2)
+        y_group(0, 512, 256, on_scalar)
         y_quant(0, 0, 512)
-        turn_y(0, 512, 0, 2)
         y_quant(0, 512, 256)
+        turn_y(0, 512, 0, 2)
         store_words(0, 0, 768)
         store_scales(0, [nc.sync] * 4)
         p_product(1, 256, 256, 2)
         y_group(1, 0, 256, on_scalar)
+        p_product(1, 512, 128, 4)
         y_group(1, 256, 256, on_vector)
         y_quant(1, 0, 256)
         turn_y(1, 0, 0, 2)
-        y_quant(1, 256, 256)
-        store_words(1, 0, 512)
-        p_product(1, 512, 128, 4)
         turn_y(1, 256, 0, 2)
         p_product(1, 640, 128, 1)
+        y_quant(1, 256, 256)
+        store_words(1, 0, 512)
+        turn_y(1, 512, 0, 1)
         y_group(1, 512, 128, on_vector)
         y_group(1, 640, 128, on_vector)
-        turn_y(1, 512, 0, 1)
         y_quant(1, 512, 128)
         y_quant(1, 640, 128)
         store_words(1, 512, 256)

@@ -18,18 +18,18 @@ COPY = mybir.ActivationFunctionType.Copy
 
 P = 128
 SLOTS = 4
-PASS = 512
+PASS = P * SLOTS
+BANK = 512
+HALF = BANK // 2
 DG = D // PASS
 RG = R // PASS
-BANK = 512
-S_MAIN = 512
-S_TAIL = S - S_MAIN
-B_SCALE_PARTS = ((0, 1), (1, 2))
+VEC_ROWS = 16
+
 MIX_COL = (PASS, 0)
 Z_COL = D
-HALF = PASS // 2
 MOVING = D + S
-QF = 2
+
+B_SCALE_PARTS = ((0, 1), (1, 2))
 
 
 def tile_clipped_flux_reprojection_k4_kernel(
@@ -37,6 +37,7 @@ def tile_clipped_flux_reprojection_k4_kernel(
     out_0, out_1, out_2,
 ):
     nc = tc.nc
+    on_vector, on_scalar = nc.vector.tensor_copy, nc.scalar.copy
     with ExitStack() as ctx:
         keep = ctx.enter_context(tc.tile_pool(name="keep", bufs=1))
         work = ctx.enter_context(tc.tile_pool(name="work", bufs=2))
@@ -50,14 +51,12 @@ def tile_clipped_flux_reprojection_k4_kernel(
             return psum.tile(shape, F32, name="bank")
 
         ident = kept("ident", [P, P], F32)
-        warm = kept("warm", [P, 8], F32)
         vec_rows = kept("vec_rows", [P, PASS], BF16)
         vec_sorted = kept("vec_sorted", [P, SLOTS, P], F32)
-        react = kept("react", [P, 16, SLOTS], F32)
+        react = kept("react", [P, VEC_ROWS, SLOTS], F32)
         gain_sb = kept("gain_sb", [P, DG, SLOTS], BF16)
         step_bf = kept("step_bf", [P, DG, SLOTS], BF16)
         step_sb = kept("step_sb", [P, DG, SLOTS], F32)
-        mix_raw = {0: kept("mix_raw", [P, SLOTS, D], BF16)}
         moves_raw = kept("moves_raw", [P, S // P, D], BF16)
         b_raw = [kept("b_raw%d" % g, [P, DG * 2 * PASS], U8) for g in range(RG)]
         b_codes = [kept("b_codes%d" % g, [P, SLOTS, DG * 2 * P], U8) for g in range(RG)]
@@ -72,14 +71,8 @@ def tile_clipped_flux_reprojection_k4_kernel(
         y_codes = kept("y_codes", [P, DG, S], U32)
         y_sc = kept("y_sc", [P, DG, S], U8)
         shift = kept("shift", [P, DG, SLOTS, S], F32)
-        mix_grouped = {}
         live = {}
 
-        def interleave(dst, src, copy=nc.vector.tensor_copy):
-            copy(
-                out=dst.rearrange("p (c i t) -> p c t i", i=4, t=SLOTS),
-                in_=src.rearrange("p t (c i) -> p c t i", i=4),
-            )
 
         def load_scales(dst, src):
             for q in range(4):
@@ -94,21 +87,21 @@ def tile_clipped_flux_reprojection_k4_kernel(
                 in_=b_words[:, :, 2 * PASS * g : 2 * PASS * (g + 1)].bitcast(I32).rearrange("k p n -> p k n"),
             )
 
-        def load_z(s0, n):
-            nc.sync.dma_start(
-                out=mov_codes[:, :, Z_COL + s0 : Z_COL + s0 + n].bitcast(I32),
-                in_=z_words.rearrange("k p n t -> p k (n t)").bitcast(I32)[:, :, s0 : s0 + n],
+        def load_b_scales(part):
+            g0, n = B_SCALE_PARTS[part]
+            load_scales(
+                bs_raw[part][:].rearrange("p (k n) -> p k n", k=DG), b_scales[:, :, PASS * g0 : PASS * (g0 + n)]
             )
 
         def load_vector(i, vec, queue):
             queue.dma_start(out=vec_rows[RG * i : RG * (i + 1), :], in_=vec.rearrange("(g r) -> g r", g=RG))
 
-        def mix_rows(h):
-            return mix[PASS * h : PASS * (h + 1), :].rearrange("(p t) k -> p t k", t=SLOTS)
+        def load_mix(h, t0, t1):
+            if t0 == 0:
+                live["mix_raw", h] = kept("mix_raw", [P, SLOTS, D], BF16)
+            rows = mix[PASS * h : PASS * (h + 1), :].rearrange("(p t) k -> p t k", t=SLOTS)
+            nc.sync.dma_start(out=live["mix_raw", h][:, t0:t1, :], in_=rows[:, t0:t1, :])
 
-        def load_late_mix():
-            mix_raw[1] = kept("mix_raw", [P, SLOTS, D], BF16)
-            nc.sync.dma_start(out=mix_raw[1][:], in_=mix_rows(1))
 
         def sort_b(g):
             nc.vector.tensor_copy(
@@ -116,77 +109,106 @@ def tile_clipped_flux_reprojection_k4_kernel(
                 in_=b_raw[g][:].bitcast(I32).rearrange("p (m t j) -> p t m j", t=SLOTS, j=4),
             )
 
-        def load_b_scales(i):
-            g0, n = B_SCALE_PARTS[i]
-            load_scales(bs_raw[i][:].rearrange("p (k n) -> p k n", k=DG), b_scales[:, :, PASS * g0 : PASS * (g0 + n)])
-
-        def sort_b_scales(i):
+        def sort_b_scales(part):
             nc.vector.tensor_copy(
-                out=b_sc[i][:].bitcast(I32).rearrange("p t (m j) -> p t m j", j=2),
-                in_=bs_raw[i][:].bitcast(I32).rearrange("p (m t j) -> p t m j", t=SLOTS, j=2),
+                out=b_sc[part][:].bitcast(I32).rearrange("p t (m j) -> p t m j", j=2),
+                in_=bs_raw[part][:].bitcast(I32).rearrange("p (m t j) -> p t m j", t=SLOTS, j=2),
             )
 
         def sort_vectors():
-            nc.vector.tensor_copy(
+            nc.scalar.activation(
                 out=vec_sorted[:].rearrange("p t (b i) -> p t b i", i=8),
                 in_=vec_rows[:].rearrange("p (b t i) -> p t b i", t=SLOTS, i=8),
+                func=COPY,
             )
 
         def turn_vectors():
             acc = bank([P, SLOTS, P])
             for t in range(SLOTS):
                 nc.tensor.transpose(acc[:, t, :], vec_sorted[:, t, :], ident[:])
-            nc.vector.tensor_copy(out=react[:], in_=acc[:, :, 0:16].rearrange("p t r -> p r t"))
+            nc.vector.tensor_copy(out=react[:], in_=acc[:, :, 0:VEC_ROWS].rearrange("p t r -> p r t"))
 
-        def sort_words(dst, src, copy):
+
+        def sort_words(key, rows, copy):
+            words = work.tile([P, PASS], F32, name="sorted_words", bufs=S // P)
+            live[key] = words
             copy(
-                out=dst.rearrange("p (k u c) -> p k u c", k=DG, u=2),
-                in_=src.bitcast(F32).rearrange("p (k c u) -> p k u c", k=DG, u=2),
+                out=words[:].rearrange("p (k u c) -> p k u c", k=DG, u=2),
+                in_=rows.bitcast(F32).rearrange("p (k c u) -> p k u c", k=DG, u=2),
             )
 
-        def sort_mix(h, t, copy=nc.vector.tensor_copy):
-            words = work.tile([P, PASS], F32, name="sorted_words", bufs=6)
-            live["mix_words", h, t] = words
-            sort_words(words[:], mix_raw[h][:, t, :], copy)
+        def sort_mix(h, t, copy):
+            sort_words(("mix_words", h, t), live["mix_raw", h][:, t, :], copy)
 
-        def sort_moves(j, copy=nc.vector.tensor_copy):
-            words = work.tile([P, PASS], F32, name="sorted_words", bufs=6)
-            live["moves_words", j] = words
-            sort_words(words[:], moves_raw[:, j, :], copy)
+        def sort_moves(j):
+            sort_words(("moves_words", j), moves_raw[:, j, :], on_vector)
 
-        def turn_mix(h, t, copy):
-            if h not in mix_grouped:
-                mix_grouped[h] = keep.tile([P, DG, SLOTS * PASS], BF16, name="mix_grouped", align_bytes=64)
+        def sorted_words(key, k, u):
+            return live[key][:, P * (2 * k + u) : P * (2 * k + u + 1)]
+
+        def turn_mix(h, t):
+            if t == 0:
+                live["mix_grouped", h] = kept("mix_grouped", [P, DG, SLOTS * PASS], BF16)
             acc = bank([P, DG, 2, P])
             for k in range(DG):
                 for u in range(2):
-                    if ("mix_words", h, t) in live:
-                        src = live["mix_words", h, t][:, P * (2 * k + u) : P * (2 * k + u + 1)]
+                    if (h, t) == (0, 0):
+                        src = live["mix_raw", h][:, t, :].bitcast(F32)[:, 2 * P * k + u : 2 * P * (k + 1) : 2]
                     else:
-                        src = mix_raw[h][:, t, :].bitcast(F32)[:, 256 * k + u : 256 * (k + 1) : 2]
+                        src = sorted_words(("mix_words", h, t), k, u)
                     nc.tensor.transpose(acc[:, k, u, :], src, ident[:])
-            dst = mix_grouped[h][:].bitcast(F32).rearrange("p k (c u) -> p k c u", u=2)
-            copy(out=dst[:, :, P * t : P * (t + 1), :], in_=acc[:].rearrange("p k u c -> p k c u"))
+            dst = live["mix_grouped", h][:].bitcast(F32).rearrange("p k (c u) -> p k c u", u=2)
+            nc.scalar.copy(out=dst[:, :, P * t : P * (t + 1), :], in_=acc[:].rearrange("p k u c -> p k c u"))
 
-        def quant_mix(h, k, c0, n):
+        def quant_mix(h, c0, n):
             cols = slice(MIX_COL[h] + c0, MIX_COL[h] + c0 + n)
-            nc.vector.quantize_mx(
-                out=mov_codes[:, k, cols].bitcast(FP8X4),
-                scales=mov_sc[:, k, cols],
-                in_=mix_grouped[h][:, k, SLOTS * c0 : SLOTS * (c0 + n)],
+            for k in range(DG):
+                nc.vector.quantize_mx(
+                    out=mov_codes[:, k, cols].bitcast(FP8X4),
+                    scales=mov_sc[:, k, cols],
+                    in_=live["mix_grouped", h][:, k, SLOTS * c0 : SLOTS * (c0 + n)],
+                )
+
+        def scale_moves(h, u, s0, n, acc):
+            pairs = acc.bitcast(BF16).rearrange("p (s e) -> p e s", e=2)
+            for e in range(2):
+                t = 2 * u + e
+                nc.scalar.activation(
+                    out=shift[:, h, t, s0 : s0 + n], in_=pairs[:, e, :], func=COPY, scale=step_sb[:, h, t : t + 1]
+                )
+
+        def turn_moves(h):
+            for u in range(2):
+                acc = bank([P, BANK])
+                for j in range(BANK // P):
+                    nc.tensor.transpose(acc[:, P * j : P * (j + 1)], sorted_words(("moves_words", j), h, u), ident[:])
+                scale_moves(h, u, 0, BANK, acc[:])
+            acc = bank([P, 2, HALF])
+            for u in range(2):
+                for j in range(HALF // P):
+                    src = sorted_words(("moves_words", BANK // P + j), h, u)
+                    nc.tensor.transpose(acc[:, u, P * j : P * (j + 1)], src, ident[:])
+            for u in range(2):
+                scale_moves(h, u, BANK, HALF, acc[:, u, :])
+
+
+        def interleave(dst, src, copy):
+            copy(
+                out=dst.rearrange("p (c i t) -> p c t i", i=4, t=SLOTS),
+                in_=src.rearrange("p t (c i) -> p c t i", i=4),
             )
 
-        def times_b(dst, g, t, cols):
+        def times_b(dst, g, t, c0, n):
             part = min(g, 1)
-            g0, n = B_SCALE_PARTS[part]
+            g0, groups = B_SCALE_PARTS[part]
             for k in range(DG):
-                m = k * n + g - g0
+                m = k * groups + g - g0
                 nc.tensor.matmul_mx(
                     out=dst,
                     lhsT=b_codes[g][:, t, 2 * P * k : 2 * P * (k + 1)].bitcast(FP4X4),
                     lhsT_scale=b_sc[part][:, t, P * m : P * (m + 1)],
-                    rhs=mov_codes[:, k, cols].bitcast(FP8X4),
-                    rhs_scale=mov_sc[:, k, cols],
+                    rhs=mov_codes[:, k, c0 : c0 + n].bitcast(FP8X4),
+                    rhs_scale=mov_sc[:, k, c0 : c0 + n],
                     start=(k == 0),
                     stop=(k == DG - 1),
                 )
@@ -194,20 +216,21 @@ def tile_clipped_flux_reprojection_k4_kernel(
         def weigh(dst, src, g, t):
             nc.scalar.activation(out=dst, in_=src, func=COPY, scale=react[:, g, t : t + 1])
 
-        def q_narrow_mm(g, c):
+        def new_q_grouped(h, g):
+            live["q_grouped", h, g] = work.tile([P, SLOTS * PASS], BF16, name="q_grouped", align_bytes=64, bufs=3)
+
+        def q_narrow(g, c):
             acc = bank([P, SLOTS, P])
             live["q_narrow", g, c] = acc
-            c0 = MIX_COL[0] + P * c
             for t in range(SLOTS):
-                times_b(acc[:, t, :], g, t, slice(c0, c0 + P))
+                times_b(acc[:, t, :], g, t, MIX_COL[0] + P * c, P)
 
         def q_narrow_out(g, c):
-            if ("q_grouped", 0, g) not in live:
-                live["q_grouped", 0, g] = work.tile([P, SLOTS * PASS], BF16, name="q_grouped", align_bytes=64, bufs=3)
-            acc = live["q_narrow", g, c]
+            if c == 0:
+                new_q_grouped(0, g)
             nc.vector.tensor_tensor(
                 out=live["q_grouped", 0, g][:, BANK * c : BANK * (c + 1)].rearrange("p (n t) -> p n t", t=SLOTS),
-                in0=acc[:].rearrange("p t n -> p n t"),
+                in0=live["q_narrow", g, c][:].rearrange("p t n -> p n t"),
                 in1=react[:, g : g + 1, :].to_broadcast([P, P, SLOTS]),
                 op=ALU.mult,
             )
@@ -223,7 +246,7 @@ def tile_clipped_flux_reprojection_k4_kernel(
             live["q_rows", 0, g] = q_rows
             for t in range(SLOTS):
                 acc = bank([P, BANK])
-                times_b(acc[:], g, t, slice(Z_COL - HALF, Z_COL + HALF))
+                times_b(acc[:], g, t, Z_COL - HALF, BANK)
                 weigh(q_rows[:, t, :], acc[:, :HALF], g, t)
                 nc.scalar.copy(out=v_rows[:, t, :HALF], in_=acc[:, HALF:])
 
@@ -231,26 +254,22 @@ def tile_clipped_flux_reprojection_k4_kernel(
             v_rows = v_rows_of(g)
             for t in range(SLOTS):
                 acc = bank([P, BANK])
-                times_b(acc[:], g, t, slice(Z_COL + HALF, MOVING))
+                times_b(acc[:], g, t, Z_COL + HALF, BANK)
                 nc.scalar.copy(out=v_rows[:, t, HALF:], in_=acc[:])
 
         def q_product(g):
-            rows = work.tile([P, SLOTS, PASS], BF16, name="q_rows", align_bytes=64)
-            live["q_rows", 1, g] = rows
+            q_rows = work.tile([P, SLOTS, PASS], BF16, name="q_rows", align_bytes=64)
+            live["q_rows", 1, g] = q_rows
             for t in range(SLOTS):
                 acc = bank([P, BANK])
-                times_b(acc[:], g, t, slice(MIX_COL[1], MIX_COL[1] + PASS))
-                weigh(rows[:, t, :], acc[:], g, t)
+                times_b(acc[:], g, t, MIX_COL[1], BANK)
+                weigh(q_rows[:, t, :], acc[:], g, t)
 
         def q_group(h, g):
-            if h == 0:
-                if ("q_grouped", 0, g) not in live:
-                    live["q_grouped", 0, g] = work.tile([P, SLOTS * PASS], BF16, name="q_grouped", align_bytes=64, bufs=3)
-                interleave(live["q_grouped", 0, g][:, SLOTS * HALF :], live["q_rows", 0, g][:])
-            else:
-                grouped = work.tile([P, SLOTS * PASS], BF16, name="q_grouped", align_bytes=64, bufs=3)
-                live["q_grouped", 1, g] = grouped
-                interleave(grouped[:], live["q_rows", 1, g][:])
+            if h == 1:
+                new_q_grouped(h, g)
+            done = (SLOTS * HALF, 0)[h]
+            interleave(live["q_grouped", h, g][:, done:], live["q_rows", h, g][:], on_vector)
 
         def q_quant(h, g):
             cols = slice(PASS * h, PASS * (h + 1))
@@ -259,11 +278,11 @@ def tile_clipped_flux_reprojection_k4_kernel(
             )
 
         def v_clip(g):
-            rows = work.tile([P, SLOTS, S], BF16, name="v_clipped", align_bytes=64)
-            live["v_clipped", g] = rows
+            clipped = work.tile([P, SLOTS, S], BF16, name="v_clipped", align_bytes=64)
+            live["v_clipped", g] = clipped
             for t in range(SLOTS):
                 nc.vector.tensor_scalar(
-                    out=rows[:, t, :], in0=live["v_rows", g][:, t, :],
+                    out=clipped[:, t, :], in0=live["v_rows", g][:, t, :],
                     scalar1=react[:, RG + g, t : t + 1], scalar2=react[:, 2 * RG + g, t : t + 1],
                     op0=ALU.max, op1=ALU.min,
                 )
@@ -271,7 +290,7 @@ def tile_clipped_flux_reprojection_k4_kernel(
         def v_group(g):
             grouped = work.tile([P, SLOTS * S], BF16, name="v_grouped", align_bytes=64)
             live["v_grouped", g] = grouped
-            interleave(grouped[:], live["v_clipped", g][:])
+            interleave(grouped[:], live["v_clipped", g][:], on_vector)
 
         def v_quant(g):
             for c0, c1 in ((0, HALF), (HALF, S)):
@@ -280,37 +299,10 @@ def tile_clipped_flux_reprojection_k4_kernel(
                     in_=live["v_grouped", g][:, SLOTS * c0 : SLOTS * c1],
                 )
 
-        def scale_moves(h, u, s0, n, acc):
-            pairs = acc.bitcast(BF16).rearrange("p (s e) -> p e s", e=2)
-            for e in range(2):
-                t = 2 * u + e
-                nc.scalar.activation(
-                    out=shift[:, h, t, s0 : s0 + n], in_=pairs[:, e, :], func=COPY, scale=step_sb[:, h, t : t + 1]
-                )
-
-        def turn_moves_into(dst, h, u, j):
-            if ("moves_words", j) in live:
-                src = live["moves_words", j][:, P * (2 * h + u) : P * (2 * h + u + 1)]
-            else:
-                src = moves_raw[:, j, :].bitcast(F32)[:, 256 * h + u : 256 * (h + 1) : 2]
-            nc.tensor.transpose(dst, src, ident[:])
-
-        def turn_moves_main(h, u):
-            acc = bank([P, BANK])
-            for j in range(S_MAIN // P):
-                turn_moves_into(acc[:, P * j : P * (j + 1)], h, u, j)
-            scale_moves(h, u, 0, S_MAIN, acc[:])
-
-        def turn_moves_tail(h):
-            acc = bank([P, 2, S_TAIL])
-            for u in range(2):
-                for j in range(S_TAIL // P):
-                    turn_moves_into(acc[:, u, P * j : P * (j + 1)], h, u, S_MAIN // P + j)
-            for u in range(2):
-                scale_moves(h, u, S_MAIN, S_TAIL, acc[:, u, :])
 
         def p_product(h, s0, n, per_bank):
-            y_t = work.tile([P, SLOTS, n], F32, name="y_t%d" % (n // BANK), align_bytes=64, bufs=3 - 2 * (n // BANK))
+            wide = n // BANK
+            y_t = work.tile([P, SLOTS, n], F32, name="y_t%d" % wide, align_bytes=64, bufs=(3, 1)[wide])
             live["y_t", h, s0] = y_t
             cols = slice(s0, s0 + n)
             for t0 in range(0, SLOTS, per_bank):
@@ -355,76 +347,77 @@ def tile_clipped_flux_reprojection_k4_kernel(
                     in_=y_sc[32 * q : 32 * q + 4, h, :].bitcast(I32),
                 )
 
-        def turn_y(h, s0, j0, count, copy=nc.scalar.copy):
-            for j in range(j0, j0 + count):
+        def turn_y(h, s0, n):
+            for c0 in range(0, n, P):
                 rows = work.tile([P, PASS], F32, name="y_rows", align_bytes=64, bufs=6)
                 acc = bank([P, SLOTS, P])
                 for t in range(SLOTS):
-                    nc.tensor.transpose(acc[:, t, :], live["y_t", h, s0][:, t, P * j : P * (j + 1)], ident[:])
-                copy(out=rows[:].rearrange("s (p t) -> s p t", t=SLOTS), in_=acc[:].rearrange("s t p -> s p t"))
-                r0 = s0 + P * j
-                nc.sync.dma_start(out=out_0[r0 : r0 + P, PASS * h : PASS * (h + 1)], in_=rows[:])
+                    nc.tensor.transpose(acc[:, t, :], live["y_t", h, s0][:, t, c0 : c0 + P], ident[:])
+                nc.scalar.copy(
+                    out=rows[:].rearrange("s (p t) -> s p t", t=SLOTS), in_=acc[:].rearrange("s t p -> s p t")
+                )
+                nc.sync.dma_start(out=out_0[s0 + c0 : s0 + c0 + P, PASS * h : PASS * (h + 1)], in_=rows[:])
 
-        on_vector, on_scalar = nc.vector.tensor_copy, nc.scalar.copy
+
         nc.vector.memset(vec_rows[:], 0.0)
         make_identity(nc, ident[:])
-        nc.vector.memset(warm[:], 0.0)
         nc.vector.memset(bs_raw[0][:].bitcast(I32), 0)
         nc.vector.memset(mov_sc[:, :, Z_COL:].bitcast(I32), 0)
         nc.vector.memset(bs_raw[1][:].bitcast(I32), 0)
-        nc.scalar.activation(out=warm[:, 0:1], in_=warm[:, 1:2], func=COPY, scale=warm[:, 2:3])
-        load_vector(0, react_weight, nc.gpsimd)
+
         load_vector(1, lower, nc.gpsimd)
         load_vector(2, upper, nc.gpsimd)
-        nc.sync.dma_start(out=mix_raw[0][:, 0, :], in_=mix_rows(0)[:, 0, :])
-        nc.sync.dma_start(out=mix_raw[0][:, 1, :], in_=mix_rows(0)[:, 1, :])
+        load_mix(0, 0, 1)
+        load_mix(0, 1, 2)
         load_b(0)
         load_b_scales(0)
+        load_vector(0, react_weight, nc.sync)
+        load_mix(0, 2, 3)
+        load_mix(0, 3, 4)
+        nc.sync.dma_start(
+            out=mov_codes[:, :, Z_COL:].bitcast(I32), in_=z_words.rearrange("k p n t -> p k (n t)").bitcast(I32)
+        )
         load_scales(mov_sc[:, :, Z_COL:], z_scales)
-        nc.sync.dma_start(out=mix_raw[0][:, 2, :], in_=mix_rows(0)[:, 2, :])
-        nc.sync.dma_start(out=mix_raw[0][:, 3, :], in_=mix_rows(0)[:, 3, :])
-        load_z(0, S)
 
-        turn_mix(0, 0, on_scalar)
-        sort_mix(0, 1)
-        turn_mix(0, 1, on_scalar)
+        turn_mix(0, 0)
+        sort_mix(0, 1, on_vector)
+        turn_mix(0, 1)
         sort_b(0)
         sort_b_scales(0)
-        quant_mix(0, 0, 0, P)
-        quant_mix(0, 1, 0, P)
+        quant_mix(0, 0, P)
+        quant_mix(0, P, P)
+        q_narrow(0, 0)
+        sort_mix(0, 2, on_vector)
+        sort_mix(0, 3, on_vector)
         sort_vectors()
-        quant_mix(0, 0, P, P)
-        quant_mix(0, 1, P, P)
-        q_narrow_mm(0, 0)
-        sort_mix(0, 2)
-        sort_mix(0, 3)
-        turn_mix(0, 2, on_scalar)
-        turn_mix(0, 3, on_scalar)
+        turn_mix(0, 2)
+        turn_mix(0, 3)
         load_b_scales(1)
         load_b(1)
         load_b(2)
-        load_late_mix()
+        load_mix(1, 0, SLOTS)
         nc.sync.dma_start(out=step_bf[:], in_=step.rearrange("(h p t) -> p h t", h=DG, t=SLOTS))
         nc.sync.dma_start(out=gain_sb[:], in_=gain.rearrange("(h p t) -> p h t", h=DG, t=SLOTS))
         nc.sync.dma_start(out=moves_raw[:], in_=moves.rearrange("(j s) d -> s j d", s=P))
         turn_vectors()
+
         q_narrow_out(0, 0)
-        q_narrow_mm(0, 1)
+        q_narrow(0, 1)
         v_product(0)
         q_narrow_out(0, 1)
-        quant_mix(0, 0, 2 * P, 2 * P)
-        quant_mix(0, 1, 2 * P, 2 * P)
+        quant_mix(0, HALF, HALF)
         sort_b(1)
         sort_b(2)
         sort_b_scales(1)
         shared_product(0)
         sort_mix(1, 2, on_scalar)
         sort_mix(1, 3, on_scalar)
-        sort_mix(1, 0)
-        sort_mix(1, 1)
+        sort_mix(1, 0, on_vector)
+        sort_mix(1, 1, on_vector)
         nc.vector.tensor_copy(out=step_sb[:], in_=step_bf[:])
-        q_narrow_mm(1, 0)
-        q_narrow_mm(1, 1)
+
+        q_narrow(1, 0)
+        q_narrow(1, 1)
         shared_product(1)
         v_clip(0)
         q_narrow_out(1, 0)
@@ -432,23 +425,21 @@ def tile_clipped_flux_reprojection_k4_kernel(
         q_group(0, 0)
         v_product(1)
         v_group(0)
-        turn_mix(1, 0, on_scalar)
-        turn_mix(1, 1, on_scalar)
-        turn_mix(1, 2, on_scalar)
-        turn_mix(1, 3, on_scalar)
+        for t in range(SLOTS):
+            turn_mix(1, t)
         sort_moves(0)
         sort_moves(1)
         v_quant(0)
         v_clip(1)
         q_group(0, 1)
         q_quant(0, 0)
-        q_narrow_mm(2, 0)
-        q_narrow_mm(2, 1)
+
+        q_narrow(2, 0)
+        q_narrow(2, 1)
         sort_moves(2)
         sort_moves(3)
         q_narrow_out(2, 0)
-        quant_mix(1, 0, 0, PASS)
-        quant_mix(1, 1, 0, PASS)
+        quant_mix(1, 0, PASS)
         sort_moves(4)
         sort_moves(5)
         q_narrow_out(2, 1)
@@ -460,50 +451,46 @@ def tile_clipped_flux_reprojection_k4_kernel(
         q_quant(0, 1)
         v_quant(1)
         v_group(2)
+
         q_product(0)
         q_quant(0, 2)
         v_quant(2)
         q_product(1)
-        turn_moves_main(0, 0)
-        turn_moves_main(0, 1)
-        turn_moves_tail(0)
+        turn_moves(0)
         q_group(1, 0)
         q_group(1, 1)
         q_product(2)
         p_product(0, 0, 512, 1)
-        turn_moves_main(1, 0)
-        turn_moves_main(1, 1)
-        turn_moves_tail(1)
-        turn_y(0, 0, 0, 2)
-        turn_y(0, 0, 2, 2)
+        turn_moves(1)
+        turn_y(0, 0, 512)
         q_group(1, 2)
-        q_quant(1, 0)
-        q_quant(1, 1)
-        q_quant(1, 2)
+        for g in range(RG):
+            q_quant(1, g)
+
         p_product(0, 512, 256, 2)
         y_group(0, 0, 512, on_vector)
         p_product(1, 0, 256, 2)
         y_group(0, 512, 256, on_scalar)
         y_quant(0, 0, 512)
         y_quant(0, 512, 256)
-        turn_y(0, 512, 0, 2)
-        store_words(0, 0, 768)
+        turn_y(0, 512, 256)
+        store_words(0, 0, S)
         store_scales(0, [nc.sync] * 4)
         p_product(1, 256, 256, 2)
         y_group(1, 0, 256, on_scalar)
         p_product(1, 512, 128, 4)
         y_group(1, 256, 256, on_vector)
         y_quant(1, 0, 256)
-        turn_y(1, 0, 0, 2)
-        turn_y(1, 256, 0, 2)
+        turn_y(1, 0, 256)
+        turn_y(1, 256, 256)
         p_product(1, 640, 128, 1)
         y_quant(1, 256, 256)
         store_words(1, 0, 512)
-        turn_y(1, 512, 0, 1)
+        turn_y(1, 512, 128)
         y_group(1, 512, 128, on_vector)
         y_group(1, 640, 128, on_vector)
         y_quant(1, 512, 128)
         y_quant(1, 640, 128)
         store_words(1, 512, 256)
-        turn_y(1, 640, 0, 1)
+        turn_y(1, 640, 128)
         store_scales(1, [nc.scalar, nc.sync] * 2)

from contextlib import ExitStack

import concourse.mybir as mybir
from concourse.masks import make_identity

S, D, R = 768, 1024, 1536
FLOPS = 2 * S * D * R + 2 * D * D * R + 2 * S * R * D

F32 = mybir.dt.float32
BF16 = mybir.dt.bfloat16
I32 = mybir.dt.int32
U32 = mybir.dt.uint32
U8 = mybir.dt.uint8
FP8X4 = mybir.dt.float8_e4m3fn_x4
FP4X4 = mybir.dt.float4_e2m1fn_x4
ALU = mybir.AluOpType
COPY = mybir.ActivationFunctionType.Copy

P = 128
SLOTS = 4
PASS = P * SLOTS
BANK = 512
HALF = BANK // 2
DG = D // PASS
RG = R // PASS
VEC_ROWS = 16

MIX_COL = (PASS, 0)
Z_COL = D
MOVING = D + S

B_SCALE_PARTS = ((0, 1), (1, 2))


def tile_clipped_flux_reprojection_k4_kernel(
    tc, z_words, z_scales, b_words, b_scales, mix, lower, upper, react_weight, gain, step, moves,
    out_0, out_1, out_2,
):
    nc = tc.nc
    on_vector, on_scalar = nc.vector.tensor_copy, nc.scalar.copy
    with ExitStack() as ctx:
        keep = ctx.enter_context(tc.tile_pool(name="keep", bufs=1))
        work = ctx.enter_context(tc.tile_pool(name="work", bufs=2))
        psum = ctx.enter_context(tc.psum_pool(name="psum", bufs=8))
        ctx.enter_context(tc.manual_schedule())

        def kept(name, shape, dtype):
            return keep.tile(shape, dtype, name=name, align_bytes=64)

        def bank(shape):
            return psum.tile(shape, F32, name="bank")

        ident = kept("ident", [P, P], F32)
        vec_rows = kept("vec_rows", [P, PASS], BF16)
        vec_sorted = kept("vec_sorted", [P, SLOTS, P], F32)
        react = kept("react", [P, VEC_ROWS, SLOTS], F32)
        gain_sb = kept("gain_sb", [P, DG, SLOTS], BF16)
        step_bf = kept("step_bf", [P, DG, SLOTS], BF16)
        step_sb = kept("step_sb", [P, DG, SLOTS], F32)
        moves_raw = kept("moves_raw", [P, S // P, D], BF16)
        b_raw = [kept("b_raw%d" % g, [P, DG * 2 * PASS], U8) for g in range(RG)]
        b_codes = [kept("b_codes%d" % g, [P, SLOTS, DG * 2 * P], U8) for g in range(RG)]
        bs_raw = [kept("bs_raw%d" % i, [P, DG * PASS * n], U8) for i, (g0, n) in enumerate(B_SCALE_PARTS)]
        b_sc = [kept("b_sc%d" % i, [P, SLOTS, DG * P * n], U8) for i, (g0, n) in enumerate(B_SCALE_PARTS)]
        mov_codes = kept("mov_codes", [P, DG, MOVING], U32)
        mov_sc = kept("mov_sc", [P, DG, MOVING], U8)
        q_codes = kept("q_codes", [P, RG, D], U32)
        q_sc = kept("q_sc", [P, RG, D], U8)
        v_codes = kept("v_codes", [P, RG, S], U32)
        v_sc = kept("v_sc", [P, RG, S], U8)
        y_codes = kept("y_codes", [P, DG, S], U32)
        y_sc = kept("y_sc", [P, DG, S], U8)
        shift = kept("shift", [P, DG, SLOTS, S], F32)
        live = {}


        def load_scales(dst, src):
            for q in range(4):
                nc.sync.dma_start(
                    out=dst[32 * q : 32 * q + 4].bitcast(I32),
                    in_=src[:, 4 * q : 4 * q + 4, :].bitcast(I32).rearrange("k q n -> q k n"),
                )

        def load_b(g):
            nc.sync.dma_start(
                out=b_raw[g][:].bitcast(I32).rearrange("p (k n) -> p k n", k=DG),
                in_=b_words[:, :, 2 * PASS * g : 2 * PASS * (g + 1)].bitcast(I32).rearrange("k p n -> p k n"),
            )

        def load_b_scales(part):
            g0, n = B_SCALE_PARTS[part]
            load_scales(
                bs_raw[part][:].rearrange("p (k n) -> p k n", k=DG), b_scales[:, :, PASS * g0 : PASS * (g0 + n)]
            )

        def load_vector(i, vec, queue):
            queue.dma_start(out=vec_rows[RG * i : RG * (i + 1), :], in_=vec.rearrange("(g r) -> g r", g=RG))

        def load_mix(h, t0, t1):
            if t0 == 0:
                live["mix_raw", h] = kept("mix_raw", [P, SLOTS, D], BF16)
            rows = mix[PASS * h : PASS * (h + 1), :].rearrange("(p t) k -> p t k", t=SLOTS)
            nc.sync.dma_start(out=live["mix_raw", h][:, t0:t1, :], in_=rows[:, t0:t1, :])


        def sort_b(g):
            nc.vector.tensor_copy(
                out=b_codes[g][:].bitcast(I32).rearrange("p t (m j) -> p t m j", j=4),
                in_=b_raw[g][:].bitcast(I32).rearrange("p (m t j) -> p t m j", t=SLOTS, j=4),
            )

        def sort_b_scales(part):
            nc.vector.tensor_copy(
                out=b_sc[part][:].bitcast(I32).rearrange("p t (m j) -> p t m j", j=2),
                in_=bs_raw[part][:].bitcast(I32).rearrange("p (m t j) -> p t m j", t=SLOTS, j=2),
            )

        def sort_vectors():
            nc.scalar.activation(
                out=vec_sorted[:].rearrange("p t (b i) -> p t b i", i=8),
                in_=vec_rows[:].rearrange("p (b t i) -> p t b i", t=SLOTS, i=8),
                func=COPY,
            )

        def turn_vectors():
            acc = bank([P, SLOTS, P])
            for t in range(SLOTS):
                nc.tensor.transpose(acc[:, t, :], vec_sorted[:, t, :], ident[:])
            nc.vector.tensor_copy(out=react[:], in_=acc[:, :, 0:VEC_ROWS].rearrange("p t r -> p r t"))


        def sort_words(key, rows, copy):
            words = work.tile([P, PASS], F32, name="sorted_words", bufs=S // P)
            live[key] = words
            copy(
                out=words[:].rearrange("p (k u c) -> p k u c", k=DG, u=2),
                in_=rows.bitcast(F32).rearrange("p (k c u) -> p k u c", k=DG, u=2),
            )

        def sort_mix(h, t, copy):
            sort_words(("mix_words", h, t), live["mix_raw", h][:, t, :], copy)

        def sort_moves(j):
            sort_words(("moves_words", j), moves_raw[:, j, :], on_vector)

        def sorted_words(key, k, u):
            return live[key][:, P * (2 * k + u) : P * (2 * k + u + 1)]

        def turn_mix(h, t):
            if t == 0:
                live["mix_grouped", h] = kept("mix_grouped", [P, DG, SLOTS * PASS], BF16)
            acc = bank([P, DG, 2, P])
            for k in range(DG):
                for u in range(2):
                    if (h, t) == (0, 0):
                        src = live["mix_raw", h][:, t, :].bitcast(F32)[:, 2 * P * k + u : 2 * P * (k + 1) : 2]
                    else:
                        src = sorted_words(("mix_words", h, t), k, u)
                    nc.tensor.transpose(acc[:, k, u, :], src, ident[:])
            dst = live["mix_grouped", h][:].bitcast(F32).rearrange("p k (c u) -> p k c u", u=2)
            nc.scalar.copy(out=dst[:, :, P * t : P * (t + 1), :], in_=acc[:].rearrange("p k u c -> p k c u"))

        def quant_mix(h, c0, n):
            cols = slice(MIX_COL[h] + c0, MIX_COL[h] + c0 + n)
            for k in range(DG):
                nc.vector.quantize_mx(
                    out=mov_codes[:, k, cols].bitcast(FP8X4),
                    scales=mov_sc[:, k, cols],
                    in_=live["mix_grouped", h][:, k, SLOTS * c0 : SLOTS * (c0 + n)],
                )

        def scale_moves(h, u, s0, n, acc):
            pairs = acc.bitcast(BF16).rearrange("p (s e) -> p e s", e=2)
            for e in range(2):
                t = 2 * u + e
                nc.scalar.activation(
                    out=shift[:, h, t, s0 : s0 + n], in_=pairs[:, e, :], func=COPY, scale=step_sb[:, h, t : t + 1]
                )

        def turn_moves(h):
            for u in range(2):
                acc = bank([P, BANK])
                for j in range(BANK // P):
                    nc.tensor.transpose(acc[:, P * j : P * (j + 1)], sorted_words(("moves_words", j), h, u), ident[:])
                scale_moves(h, u, 0, BANK, acc[:])
            acc = bank([P, 2, HALF])
            for u in range(2):
                for j in range(HALF // P):
                    src = sorted_words(("moves_words", BANK // P + j), h, u)
                    nc.tensor.transpose(acc[:, u, P * j : P * (j + 1)], src, ident[:])
            for u in range(2):
                scale_moves(h, u, BANK, HALF, acc[:, u, :])


        def interleave(dst, src, copy):
            copy(
                out=dst.rearrange("p (c i t) -> p c t i", i=4, t=SLOTS),
                in_=src.rearrange("p t (c i) -> p c t i", i=4),
            )

        def times_b(dst, g, t, c0, n):
            part = min(g, 1)
            g0, groups = B_SCALE_PARTS[part]
            for k in range(DG):
                m = k * groups + g - g0
                nc.tensor.matmul_mx(
                    out=dst,
                    lhsT=b_codes[g][:, t, 2 * P * k : 2 * P * (k + 1)].bitcast(FP4X4),
                    lhsT_scale=b_sc[part][:, t, P * m : P * (m + 1)],
                    rhs=mov_codes[:, k, c0 : c0 + n].bitcast(FP8X4),
                    rhs_scale=mov_sc[:, k, c0 : c0 + n],
                    start=(k == 0),
                    stop=(k == DG - 1),
                )

        def weigh(dst, src, g, t):
            nc.scalar.activation(out=dst, in_=src, func=COPY, scale=react[:, g, t : t + 1])

        def new_q_grouped(h, g):
            live["q_grouped", h, g] = work.tile([P, SLOTS * PASS], BF16, name="q_grouped", align_bytes=64, bufs=3)

        def q_narrow(g, c):
            acc = bank([P, SLOTS, P])
            live["q_narrow", g, c] = acc
            for t in range(SLOTS):
                times_b(acc[:, t, :], g, t, MIX_COL[0] + P * c, P)

        def q_narrow_out(g, c):
            if c == 0:
                new_q_grouped(0, g)
            nc.vector.tensor_tensor(
                out=live["q_grouped", 0, g][:, BANK * c : BANK * (c + 1)].rearrange("p (n t) -> p n t", t=SLOTS),
                in0=live["q_narrow", g, c][:].rearrange("p t n -> p n t"),
                in1=react[:, g : g + 1, :].to_broadcast([P, P, SLOTS]),
                op=ALU.mult,
            )

        def v_rows_of(g):
            if ("v_rows", g) not in live:
                live["v_rows", g] = work.tile([P, SLOTS, S], BF16, name="v_rows", align_bytes=64)
            return live["v_rows", g]

        def shared_product(g):
            q_rows = work.tile([P, SLOTS, HALF], BF16, name="q_half_rows", align_bytes=64)
            v_rows = v_rows_of(g)
            live["q_rows", 0, g] = q_rows
            for t in range(SLOTS):
                acc = bank([P, BANK])
                times_b(acc[:], g, t, Z_COL - HALF, BANK)
                weigh(q_rows[:, t, :], acc[:, :HALF], g, t)
                nc.scalar.copy(out=v_rows[:, t, :HALF], in_=acc[:, HALF:])

        def v_product(g):
            v_rows = v_rows_of(g)
            for t in range(SLOTS):
                acc = bank([P, BANK])
                times_b(acc[:], g, t, Z_COL + HALF, BANK)
                nc.scalar.copy(out=v_rows[:, t, HALF:], in_=acc[:])

        def q_product(g):
            q_rows = work.tile([P, SLOTS, PASS], BF16, name="q_rows", align_bytes=64)
            live["q_rows", 1, g] = q_rows
            for t in range(SLOTS):
                acc = bank([P, BANK])
                times_b(acc[:], g, t, MIX_COL[1], BANK)
                weigh(q_rows[:, t, :], acc[:], g, t)

        def q_group(h, g):
            if h == 1:
                new_q_grouped(h, g)
            done = (SLOTS * HALF, 0)[h]
            interleave(live["q_grouped", h, g][:, done:], live["q_rows", h, g][:], on_vector)

        def q_quant(h, g):
            cols = slice(PASS * h, PASS * (h + 1))
            nc.vector.quantize_mx(
                out=q_codes[:, g, cols].bitcast(FP8X4), scales=q_sc[:, g, cols], in_=live["q_grouped", h, g][:]
            )

        def v_clip(g):
            clipped = work.tile([P, SLOTS, S], BF16, name="v_clipped", align_bytes=64)
            live["v_clipped", g] = clipped
            for t in range(SLOTS):
                nc.vector.tensor_scalar(
                    out=clipped[:, t, :], in0=live["v_rows", g][:, t, :],
                    scalar1=react[:, RG + g, t : t + 1], scalar2=react[:, 2 * RG + g, t : t + 1],
                    op0=ALU.max, op1=ALU.min,
                )

        def v_group(g):
            grouped = work.tile([P, SLOTS * S], BF16, name="v_grouped", align_bytes=64)
            live["v_grouped", g] = grouped
            interleave(grouped[:], live["v_clipped", g][:], on_vector)

        def v_quant(g):
            for c0, c1 in ((0, HALF), (HALF, S)):
                nc.vector.quantize_mx(
                    out=v_codes[:, g, c0:c1].bitcast(FP8X4), scales=v_sc[:, g, c0:c1],
                    in_=live["v_grouped", g][:, SLOTS * c0 : SLOTS * c1],
                )


        def p_product(h, s0, n, per_bank):
            wide = n // BANK
            y_t = work.tile([P, SLOTS, n], F32, name="y_t%d" % wide, align_bytes=64, bufs=(3, 1)[wide])
            live["y_t", h, s0] = y_t
            cols = slice(s0, s0 + n)
            for t0 in range(0, SLOTS, per_bank):
                acc = bank([P, per_bank, n])
                for e in range(per_bank):
                    d = slice(PASS * h + P * (t0 + e), PASS * h + P * (t0 + e + 1))
                    for g in range(RG):
                        nc.tensor.matmul_mx(
                            out=acc[:, e, :],
                            lhsT=q_codes[:, g, d].bitcast(FP8X4), lhsT_scale=q_sc[:, g, d],
                            rhs=v_codes[:, g, cols].bitcast(FP8X4), rhs_scale=v_sc[:, g, cols],
                            start=(g == 0), stop=(g == RG - 1),
                        )
                for e in range(per_bank):
                    t = t0 + e
                    nc.vector.scalar_tensor_tensor(
                        out=y_t[:, t, :], in0=acc[:, e, :], scalar=gain_sb[:, h, t : t + 1],
                        in1=shift[:, h, t, cols], op0=ALU.mult, op1=ALU.add,
                    )

        def y_group(h, s0, n, copy):
            grouped = work.tile([P, SLOTS * n], BF16, name="y_grouped", align_bytes=64)
            live["y_grouped", h, s0] = grouped
            interleave(grouped[:], live["y_t", h, s0][:], copy)

        def y_quant(h, s0, n):
            cols = slice(s0, s0 + n)
            nc.vector.quantize_mx(
                out=y_codes[:, h, cols].bitcast(FP8X4), scales=y_sc[:, h, cols], in_=live["y_grouped", h, s0][:]
            )

        def store_words(h, s0, n):
            nc.sync.dma_start(
                out=out_1[h].rearrange("p s t -> p (s t)").bitcast(I32)[:, s0 : s0 + n],
                in_=y_codes[:, h, s0 : s0 + n].bitcast(I32),
            )

        def store_scales(h, queues):
            for q in range(4):
                queues[q].dma_start(
                    out=out_2[h, 4 * q : 4 * q + 4, :].bitcast(I32),
                    in_=y_sc[32 * q : 32 * q + 4, h, :].bitcast(I32),
                )

        def turn_y(h, s0, n):
            for c0 in range(0, n, P):
                rows = work.tile([P, PASS], F32, name="y_rows", align_bytes=64, bufs=6)
                acc = bank([P, SLOTS, P])
                for t in range(SLOTS):
                    nc.tensor.transpose(acc[:, t, :], live["y_t", h, s0][:, t, c0 : c0 + P], ident[:])
                nc.scalar.copy(
                    out=rows[:].rearrange("s (p t) -> s p t", t=SLOTS), in_=acc[:].rearrange("s t p -> s p t")
                )
                nc.sync.dma_start(out=out_0[s0 + c0 : s0 + c0 + P, PASS * h : PASS * (h + 1)], in_=rows[:])


        nc.vector.memset(vec_rows[:], 0.0)
        make_identity(nc, ident[:])
        nc.vector.memset(bs_raw[0][:].bitcast(I32), 0)
        nc.vector.memset(mov_sc[:, :, Z_COL:].bitcast(I32), 0)
        nc.vector.memset(bs_raw[1][:].bitcast(I32), 0)

        load_vector(1, lower, nc.gpsimd)
        load_vector(2, upper, nc.gpsimd)
        load_mix(0, 0, 1)
        load_mix(0, 1, 2)
        load_b(0)
        load_b_scales(0)
        load_vector(0, react_weight, nc.sync)
        load_mix(0, 2, 3)
        load_mix(0, 3, 4)
        nc.sync.dma_start(
            out=mov_codes[:, :, Z_COL:].bitcast(I32), in_=z_words.rearrange("k p n t -> p k (n t)").bitcast(I32)
        )
        load_scales(mov_sc[:, :, Z_COL:], z_scales)

        turn_mix(0, 0)
        sort_mix(0, 1, on_vector)
        turn_mix(0, 1)
        sort_b(0)
        sort_b_scales(0)
        quant_mix(0, 0, P)
        quant_mix(0, P, P)
        q_narrow(0, 0)
        sort_mix(0, 2, on_vector)
        sort_mix(0, 3, on_vector)
        sort_vectors()
        turn_mix(0, 2)
        turn_mix(0, 3)
        load_b_scales(1)
        load_b(1)
        load_b(2)
        load_mix(1, 0, SLOTS)
        nc.sync.dma_start(out=step_bf[:], in_=step.rearrange("(h p t) -> p h t", h=DG, t=SLOTS))
        nc.sync.dma_start(out=gain_sb[:], in_=gain.rearrange("(h p t) -> p h t", h=DG, t=SLOTS))
        nc.sync.dma_start(out=moves_raw[:], in_=moves.rearrange("(j s) d -> s j d", s=P))
        turn_vectors()

        q_narrow_out(0, 0)
        q_narrow(0, 1)
        v_product(0)
        q_narrow_out(0, 1)
        quant_mix(0, HALF, HALF)
        sort_b(1)
        sort_b(2)
        sort_b_scales(1)
        shared_product(0)
        sort_mix(1, 2, on_scalar)
        sort_mix(1, 3, on_scalar)
        sort_mix(1, 0, on_vector)
        sort_mix(1, 1, on_vector)
        nc.vector.tensor_copy(out=step_sb[:], in_=step_bf[:])

        q_narrow(1, 0)
        q_narrow(1, 1)
        shared_product(1)
        v_clip(0)
        q_narrow_out(1, 0)
        q_narrow_out(1, 1)
        q_group(0, 0)
        v_product(1)
        v_group(0)
        for t in range(SLOTS):
            turn_mix(1, t)
        sort_moves(0)
        sort_moves(1)
        v_quant(0)
        v_clip(1)
        q_group(0, 1)
        q_quant(0, 0)

        q_narrow(2, 0)
        q_narrow(2, 1)
        sort_moves(2)
        sort_moves(3)
        q_narrow_out(2, 0)
        quant_mix(1, 0, PASS)
        sort_moves(4)
        sort_moves(5)
        q_narrow_out(2, 1)
        v_group(1)
        shared_product(2)
        v_product(2)
        v_clip(2)
        q_group(0, 2)
        q_quant(0, 1)
        v_quant(1)
        v_group(2)

        q_product(0)
        q_quant(0, 2)
        v_quant(2)
        q_product(1)
        turn_moves(0)
        q_group(1, 0)
        q_group(1, 1)
        q_product(2)
        p_product(0, 0, 512, 1)
        turn_moves(1)
        turn_y(0, 0, 512)
        q_group(1, 2)
        for g in range(RG):
            q_quant(1, g)

        p_product(0, 512, 256, 2)
        y_group(0, 0, 512, on_vector)
        p_product(1, 0, 256, 2)
        y_group(0, 512, 256, on_scalar)
        y_quant(0, 0, 512)
        y_quant(0, 512, 256)
        turn_y(0, 512, 256)
        store_words(0, 0, S)
        store_scales(0, [nc.sync] * 4)
        p_product(1, 256, 256, 2)
        y_group(1, 0, 256, on_scalar)
        p_product(1, 512, 128, 4)
        y_group(1, 256, 256, on_vector)
        y_quant(1, 0, 256)
        turn_y(1, 0, 256)
        turn_y(1, 256, 256)
        p_product(1, 640, 128, 1)
        y_quant(1, 256, 256)
        store_words(1, 0, 512)
        turn_y(1, 512, 128)
        y_group(1, 512, 128, on_vector)
        y_group(1, 640, 128, on_vector)
        y_quant(1, 512, 128)
        y_quant(1, 640, 128)
        store_words(1, 512, 256)
        turn_y(1, 640, 128)
        store_scales(1, [nc.scalar, nc.sync] * 2)
